import numpy as np, ml_dtypes
CORES = [23,119,17,113]
N = 4
BF = ml_dtypes.bfloat16
def gentries(a):
    return np.ascontiguousarray(a.reshape(8, 16, -1).transpose(0, 2, 1)).reshape(8, -1)
def gtable(e):
    e = np.asarray(e); return np.ascontiguousarray(e.reshape(8, -1, 16).transpose(0, 2, 1)).reshape(128, -1).astype(np.int32)
P, L, G, RO, J = 1024, 4, 1024, 3, 2
K = L * G; W = P + K
H = P // 16; C = G // 32
B = 2 ** J + 2; Y = 16; T = 3 + B + 2 * Y
ENDS = [RO - 1, 2 * RO - 2, 2 * RO - 1, 2 * RO - 1 + B, 2 * RO - 1 + 2 * B, 2 * RO - 1 + 2 * B + 2 * Y, 2 * RO + 1 + 2 * B + 3 * Y]; X = ENDS[-1] + 1
TIES = [[28, 17, 21, 9], [41, 18, 23, 5], [42, 38, 35, 13], [44, 27, 18, 7], [45, 22, 34, 4], [45, 35, 43, 14], [49, 48, 43, 15], [52, 5, 50, 11]]
def pick(rng, top, shape, pw):
    return np.minimum((top * rng.random(shape) ** pw).astype(np.int64), top - 1)
def wiring(rng, kinds=(0, 1, 2, 3, 4, 5, 6), pw=(1.0,) * 8):
    o = np.argsort(rng.random((8, P)), axis=1); z = o[:, :16]; q = o[:, 16:16 + 8 * H].reshape(8, 4, H, 2); ex = o[:, 16 + 8 * H:16 + 8 * H + X]; k = np.arange(K)
    fa = np.zeros((N, 8, K), np.int64); fb = np.zeros((N, 8, K), np.int64); cd = np.zeros((8, K), np.int64); tp = np.zeros((8, P), np.int64)
    for g in range(8):
        w = pw[g]; tops = P + k // G * G; pairs = []
        last = np.sort(np.append(G - 512 + rng.permutation(511)[:T - 1], G - 1)); sp = (L - 1) * G + last
        fa[:, g] = pick(rng, tops, (N, K), w); fb[:, g] = pick(rng, tops, (N, K), w); cd[g] = pick(rng, P + k, K, w); tp[g] = pick(rng, W, P, w)
        for l in range(L):
            top = P + l * G; m = l * G + rng.permutation(G)
            if l == L - 1: m = l * G + np.concatenate([rng.permutation(np.setdiff1d(np.arange(G), last)), last])
            pr = np.sort(m[:14 * C].reshape(7, C, 2), axis=2)
            for j, kind in enumerate(kinds):
                n1, n2 = pr[j, :, 0], pr[j, :, 1]
                a1 = pick(rng, top, (N, C), w); b1 = pick(rng, top, (N, C), w); a2 = a1.copy(); i = rng.integers(0, H, (N, C))
                if kind == 3: i = np.tile(i[:1], (N, 1)); b1 = np.tile(z[g, rng.integers(0, 16, C)], (N, 1))
                if kind >= 2: s = q[g, (0, 1, 2, 2, 3)[kind - 2]]; a1, a2 = s[i, 0], s[i, 1]
                if kind in (1, 5): a2[rng.integers(0, N, C), np.arange(C)] = pick(rng, top, C, w)
                if kind in (2, 4, 6) and rng.random() < 0.5: fa[:, g, n1] = b1; fb[:, g, n1] = a1; fa[:, g, n2] = b1; fb[:, g, n2] = a2
                else: fa[:, g, n1] = a1; fb[:, g, n1] = b1; fa[:, g, n2] = a2; fb[:, g, n2] = b1
                cd[g, n2] = P + n1
                if kind == 4: pairs.append(pr[j])
            s = m[14 * C:18 * C]; a1 = pick(rng, top, 4 * C, w)
            fa[:, g, s] = a1; fb[:, g, s] = z[g, rng.integers(0, 16, 4 * C)]; cd[g, s] = a1
            if l > 0:
                s = m[18 * C:22 * C]; i = pick(rng, l * G, 4 * C, w)
                fa[:, g, s] = fa[:, g, i]; fb[:, g, s] = fb[:, g, i]; cd[g, s] = P + i
            s = np.sort(m[22 * C:28 * C].reshape(C, 6), axis=1)
            fa[:, g, s] = pick(rng, top, (N, C, 1), w); fb[:, g, s] = pick(rng, top, (N, C, 1), w); cd[g, s[:, 1:]] = P + s[:, :-1]
        pt = np.concatenate(pairs)
        tp[g, z[g, :4]] = z[g, :4]; tp[g, q[g, 2, :, 1]] = tp[g, q[g, 2, :, 0]]; tp[g, q[g, 3]] = P + pt[rng.integers(0, len(pt), H)]
        ua, ub, us, e, h, nr, vw, full = np.split(ex[g], ENDS); t = rng.permutation(T - 1)
        n0 = np.sort(sp[t[:2]]); n1 = np.sort(sp[t[2:2 + B]]); n2 = np.sort(sp[t[2 + B:]].reshape(Y, 2), axis=1)
        fb[:, g, sp] = z[g, rng.integers(0, 4, (N, T))]
        fa[:, g, n0] = ua[0]; fa[:, g, K - 1] = ub[0]; cd[g, n0[1]] = P + n0[0]; cd[g, K - 1] = P + n0[1]
        fa[:, g, n1] = e; cd[g, n1[1:]] = P + n1[:-1]
        fa[:, g, n2] = nr.reshape(Y, 2); cd[g, n2[:, 1]] = P + n2[:, 0]
        tp[g, ua] = np.append(ua[1:], us); tp[g, ub] = np.append(ub[1:], us); tp[g, us] = us; tp[g, e] = h; tp[g, h] = e; tp[g, nr] = nr; tp[g, full] = full
        tp[g, vw] = P + np.concatenate([[K - 1, n1[-1]], n2[:, 1]])
    return z, q, ex, fa, fb, cd, tp
def gaps(rng):
    S = 16 * N; a = 16 * rng.integers(0, N, 3) + rng.integers(0, 14, 3); b = 16 * rng.integers(0, N - 2, 3) + rng.integers(0, 16, 3); u = 2 * rng.integers(0, 8 * N, 2)
    c = [([S - 1], [1]), ([0], [1]), ([S - 16], [1]), ([a[0], a[0] + 1], [2, -1]), ([a[1], a[1] + 1], [-1, 2]), ([b[0], b[0] + 16], [2, -1]), ([b[1], b[1] + 16], [-1, 2]),
         ([u[0], u[0] + 1], [255, -1]), ([u[1], u[1] + 1], [-1, 255]), ([a[2], a[2] + 1, a[2] + 2], [1, -2, 1]), ([b[2], b[2] + 16, b[2] + 32], [1, -2, 1])]
    for i in rng.integers(0, len(TIES), 2): c.append((TIES[i], [1, 1, -1, -1]))
    for i in range(3): c.append((rng.permutation(S)[:4], [1, 1, -1, -1]))
    return c
def plant(rng, xx, z, q, ex, lo=(0,) * 8, hi=(16 * N,) * 8):
    for g in range(8):
        v = xx[g]; n0, n1 = q[g, 1, :, 0], q[g, 1, :, 1]; s = hi[g] - lo[g]
        v[:, z[g]] = 0; v[:, q[g, 0, :, 1]] = v[:, q[g, 0, :, 0]]
        v[:, n0] = np.clip(v[:, n0], 1, 254); v[:, n1] = v[:, n0]
        i = rng.integers(0, s, H); j = (i + 1 + rng.integers(0, s - 1, H)) % s; mode = rng.permutation(np.arange(H) % 4)
        v[lo[g] + i, n1] += np.where(mode < 2, 1, np.where(mode == 2, -1, 0)); v[lo[g] + j, n1] -= (mode == 1).astype(np.int64)
        ua, ub, us, e, h, nr, vw, full = np.split(ex[g], ENDS)
        i = rng.integers(0, 16 * N, RO - 1); v[i, ub] = 255 - v[i, ua]
        v[rng.integers(0, 16 * N), e] = 255 * (np.arange(B) % 2); v[:, h] = v[:, h[:1]]; v[:, full] = 255
        for j, (places, d) in enumerate(gaps(rng)):
            places = np.array(places); d = np.array(d); n = nr[2 * j:2 * j + 2]
            if rng.random() < 0.5: n = n[::-1]
            c = np.clip(v[:, n[0]], 2, 253); c[places] = np.where(d == 255, 0, c[places]); v[:, n[0]] = c
            c = c.copy(); c[places] += d; v[:, n[1]] = c
    return xx
def quiet(g, xx, z, ex, fa, fb, cd):
    v = np.zeros((N, 16, W), np.int64); v[..., :P] = xx[g].reshape(N, 16, P)
    for l in range(L):
        s = slice(l * G, (l + 1) * G)
        v[..., P + l * G:P + (l + 1) * G] = np.minimum(np.take_along_axis(v, fa[:, g, None, s], 2), 255 - np.take_along_axis(v, fb[:, g, None, s], 2))
    own = v[..., P:]; same = np.all(own == v[..., cd[g]], axis=(0, 1)); zero = np.all(own == 0, axis=(0, 1))
    cd[g] = np.where(same, np.where(zero, ex[g, -1], z[g, 0]), cd[g])
def pack(xx, fa, fb, cd, tp):
    x = np.ascontiguousarray(xx.reshape(8, N, 16, P).transpose(1, 0, 2, 3)).reshape(N, 128, P)
    return {"x": x.astype(np.float32).astype(BF), "fa": np.stack([gtable(e) for e in fa]), "fb": np.stack([gtable(e) for e in fb]), "cd": np.stack([gtable(cd)] * N), "tp": np.stack([gtable(tp)] * N)}
def setup_inputs(rng):
    z, q, ex, fa, fb, cd, tp = wiring(rng)
    return pack(plant(rng, rng.integers(0, 256, (8, 16 * N, P)), z, q, ex), fa, fb, cd, tp)
def setup_inputs_near(rng):
    z, q, ex, fa, fb, cd, tp = wiring(rng, kinds=(3, 3, 3, 3, 4, 5, 1))
    for g in range(8): tp[g, z[g]] = z[g]; tp[g, q[g, 1, :H // 2]] = q[g, 1, :H // 2]
    one = (0, N - 1, 1, N - 2); lo = [16 * one[g] if g < 4 else 0 for g in range(8)]; hi = [16 * one[g] + 16 if g < 4 else 16 * N for g in range(8)]
    xx = plant(rng, rng.integers(0, 256, (8, 16 * N, P)), z, q, ex, lo, hi)
    for g in (4, 7): quiet(g, xx, z, ex, fa, fb, cd)
    return pack(xx, fa, fb, cd, tp)
def setup_inputs_chains(rng):
    z, q, ex, fa, fb, cd, tp = wiring(rng); n = G // 32; h = n // 2
    for g in range(1, 8, 2):
        last = None
        for l in range(L):
            top = P + l * G; s = l * G + np.sort(rng.permutation(G).reshape(n, 32), axis=1)
            a = rng.integers(0, top, (N, n)); b = rng.integers(0, top, (N, n))
            if l > 0: a[:, :h] = P + last[:h]; b[:, :h] = z[g, 0]; cd[g, s[:h, 0]] = P + last[:h]
            fa[:, g, s] = a[:, :, None]; fb[:, g, s] = b[:, :, None]; cd[g, s[:, 1:]] = P + s[:, :-1]
            cut = rng.random((n, 32)) < 0.08; cut[:, 0] = False; cut[0, 16] = True; c = s[cut]
            fa[rng.integers(0, N, len(c)), g, c] = rng.integers(0, top, len(c)); last = s[:, -1]
    return pack(plant(rng, rng.integers(0, 256, (8, 16 * N, P)), z, q, ex), fa, fb, cd, tp)
def setup_inputs_flat(rng):
    z, q, ex, fa, fb, cd, tp = wiring(rng)
    xx = plant(rng, 255 * rng.integers(0, 2, (8, 16 * N, P)), z, q, ex); o = rng.permutation(8)
    xx[o[0]] = 0; xx[o[1]] = 255
    return pack(xx, fa, fb, cd, tp)
def setup_inputs_ends(rng):
    z, q, ex, fa, fb, cd, tp = wiring(rng); k = np.arange(K); tops = P + k // G * G
    fa[:, 0] = np.where(rng.random((N, K)) < 0.5, 0, tops - 1); fb[:, 0] = np.where(rng.random((N, K)) < 0.5, 0, tops - 1)
    fb[:, 1] = fa[:, 1]
    cd[2] = P + k - 1
    m = rng.random(K) < 0.5; fa[:, 3, m] = 0; fb[:, 3, m] = z[3, 0]; cd[3] = 0
    tp[4] = rng.choice(np.array([0, P - 1, P, W - 1]), P)
    cd[5] = np.where(rng.random(K) < 0.5, 0, P + k - 1); fa[:, 5] = np.where(rng.random(K) < 0.5, tops - 1, fa[:, 5])
    fa[:, 6] = tops - 1; fb[:, 6] = z[6, 0]; cd[6] = P + k - 1
    return pack(plant(rng, rng.integers(0, 256, (8, 16 * N, P)), z, q, ex), fa, fb, cd, tp)
def setup_inputs_spread(rng):
    pw = rng.permutation(np.array([0.35, 0.35, 0.6, 1.0, 1.0, 1.5, 3.0, 3.0])); z, q, ex, fa, fb, cd, tp = wiring(rng, pw=pw)
    e = np.exp2(rng.integers(-3, 4, (8, 1, P)) + rng.integers(-1, 2, (8, 16 * N, 1)))
    return pack(plant(rng, np.minimum((256 * rng.random((8, 16 * N, P)) ** e).astype(np.int64), 255), z, q, ex), fa, fb, cd, tp)
def check_inputs(d):
    bad = []; k = np.arange(K); x = np.asarray(d["x"]).astype(np.float32)
    if not (np.all(x >= 0) and np.all(x <= 255) and np.all(x == np.floor(x))): bad.append("whole numbers from 0 to 255 in x")
    for name, top in (("fa", P + k // G * G), ("fb", P + k // G * G), ("cd", P + k), ("tp", W)):
        e = np.stack([gentries(s) for s in d[name]]).astype(np.int64)
        if np.any(e < 0) or np.any(e >= top): bad.append("range of " + name)
    for name in ("cd", "tp"):
        if np.any(d[name] != d[name][:1]): bad.append(name + " alike on all ranks")
    return bad
def reference(x, fa, fb, cd, tp):
    now = x.astype(np.float32).astype(np.int32).reshape(N, 8, 16, P)
    a = np.stack([gentries(e) for e in fa]).astype(np.int64); b = np.stack([gentries(e) for e in fb]).astype(np.int64)
    c = gentries(cd[0]).astype(np.int64); taps = gentries(tp[0]).astype(np.int64)
    for rnd in range(RO):
        v = np.zeros((N, 8, 16, W), np.int32); v[..., :P] = now
        for l in range(L):
            s = slice(l * G, (l + 1) * G)
            v[..., P + l * G:P + (l + 1) * G] = np.minimum(np.take_along_axis(v, a[:, :, None, s], 3), 255 - np.take_along_axis(v, b[:, :, None, s], 3))
        differ = v[..., P:] != np.take_along_axis(v, c[None, :, None, :], 3)
        mm = np.add.reduce(np.add.reduce(differ.astype(np.int32), axis=2), axis=0)
        rep = np.tile(np.arange(W), (8, 1)); rep[:, P:] = np.where(mm == 0, c, rep[:, P:])
        for j in range(J): rep = np.take_along_axis(rep, rep, 1)
        a = np.take_along_axis(rep[None], a, 2); b = np.take_along_axis(rep[None], b, 2)
        taps = np.take_along_axis(rep, taps, 1)
        now = np.take_along_axis(v, taps[None, :, None, :], 3)
    return {"yv": v.reshape(N, 128, W).astype(np.float32).astype(BF), "ya": np.stack([gtable(e) for e in a]).astype(np.float32), "yb": np.stack([gtable(e) for e in b]).astype(np.float32),
            "yt": np.stack([gtable(taps)] * N).astype(np.float32)}

@@ -1,0 +1,394 @@
+from concourse.bass import DstId, RemoteDMATransfer
+from concourse.mybir import AluOpType, ActivationFunctionType
+
+N, P, L, G, RO = 4, 1024, 4, 1024, 3
+W = P + L * G
+Q = G // N
+BIG = 128.0
+
+SCRATCH = {}
+for _names, _cols, _dt in (
+        ("v0 v1 v2 rt0 rt1 rt2 dg", W, "bfloat16"), ("u1 u2 r3", 4096, "bfloat16"), ("nb df gw", 12 * G, "bfloat16"),
+        ("ld", 36 * Q, "bfloat16"), ("g1", G, "bfloat16"), ("gf", 6 * G, "bfloat16"), ("zw", 144, "bfloat16"),
+        ("m1 m2 md mb", 128, "bfloat16"), ("fa32 fb32 cd32", 256, "int32"), ("tp32", 64, "int32"), ("ip ipm", 8, "int32"),
+        ("fa16 fb16 cd16 xl0 xl1", 256, "uint16"), ("tp16", 64, "uint16"), ("xw", 48 * 16, "uint16"),
+        ("yas ybs", 256, "float32"), ("yts", 64, "float32"), ("oh pf cc", 8, "float32"), ("xx", 160, "float32"),
+        ("yy", 128, "float32"), ("kc", 80, "float32")):
+    for _n in _names.split():
+        SCRATCH[_n] = ("sbuf", [128, _cols], _dt)
+for _b in range(8):
+    SCRATCH["ps%d" % _b] = ("psum", [128, 512], "float32")
+
+
+def build_ops():
+    ops = {}
+
+    def op(name, kind, eng, cost, n, deps, args=(), late=(), reader=None):
+        for d in list(deps) + list(late):
+            assert d in ops, (name, d)
+        ops[name] = dict(name=name, kind=kind, eng=eng, cost=cost, n=n, deps=list(deps), late=list(late), args=args, reader=reader)
+
+    op("lx", "load", "Y", "dma", 262144, [], ("x", 0, P))
+    op("ltp", "load", "YS", "dma", 32768, [], ("tp", 0, 64))
+    for t in ("fb", "fa", "cd"):
+        op("l%s0" % t, "load", "YS", "dma", 32768, [], (t, 0, 64))
+        op("l%s1" % t, "load", "YS", "dma", 98304, [], (t, 64, 256))
+        op("c%s0" % t, "conv", "V", "c1", 64, ["l%s0" % t], (t, 0, 64))
+        op("c%s1" % t, "conv", "V", "c1", 192, ["l%s1" % t], (t, 64, 256))
+    op("ctp", "conv", "V", "c1", 64, ["ltp"], ("tp", 0, 64))
+    lst = lambda t, l: "c%s%d" % (t, min(l, 1))
+    op("iip", "iota", "G", "iota", 4, [], ("ip",))
+    op("ipf", "iota", "G", "iota", 1, [], ("pf",))
+    op("ixx", "iota", "G", "iota", 146, [], ("xx",))
+    op("iyy", "iota", "G", "iota", 128, [], ("yy",))
+    tiny = [("ipm", ["iip"]), ("oh", ["ipm"]), ("tg", ["ipm", "ipf"]), ("d0", ["oh", "ixx"]), ("kc", ["oh", "ixx"]),
+            ("m1c", ["oh"]), ("dc", ["oh"]), ("bias", ["oh"]), ("w1", ["oh"]), ("wc", ["w1"]),
+            ("zw", ["wc", "tg", "ixx"]), ("m1", ["m1c", "ipf", "ixx"]), ("md", ["dc", "ipf", "ixx"]), ("m2", ["m1", "md"]),
+            ("mb", ["tg", "iyy"])]
+    for t, d in tiny:
+        op(t, "tiny", "V", "c1", {"zw": 143, "m1": 128, "md": 128, "m2": 256, "mb": 128, "kc": 80}.get(t, 64), d, (t,))
+    prev = "d0"
+    for s in (64, 128, 256, 512):
+        op("d%d" % s, "dbl", "VS", "ch", s, [prev, "kc"], (s, 0, s))
+        prev = "d%d" % s
+    for b in range(1, 5):
+        op("db%d" % b, "dbl", "VS", "ch", G, ["d512"], (G * b, 0, G))
+    op("irt0", "copyin", "Y", "dma", 262144, ["d512"], ("rt0",))
+    for l in range(L):
+        op("g1_%d" % l, "g1", "VS", "g", Q, [lst("cd", l)] + ["db%d" % b for b in range(1, l + 2)], (l,))
+
+    for r in range(RO):
+        inp = ["lx"] if r == 0 else ["np%d_0" % (r - 1), "np%d_1" % (r - 1)]
+        if r > 0:
+            op("iu%d" % r, "copyu", "Y", "dma", 262144, inp, (r,))
+            for t in ["rt%d" % r] + ["r3"] * (r == RO - 1):
+                op("i" + t, "copyin", "Y", "dma", 262144, ["d512", "A%d20" % (r - 1)], (t,))
+        src = list(inp)
+        for l in range(L):
+            rl = "%d%d" % (r, l)
+            for h in range(2):
+                op("B%s%d" % (rl, h), "B", "VS", "g", 512, src + [lst("fb", l)], (r, l, h))
+                op("A%s%d" % (rl, h), "A", "V", "tg", 512, src + [lst("fa", l), "B%s%d" % (rl, h)], (r, l, h))
+                op("cp%s%d" % (rl, h), "shadow", "YVSG", "cp", 512, ["A%s%d" % (rl, h)], (r, l, h))
+            both = ["A%s0" % rl, "A%s1" % rl]
+            low = inp + ["A%d%d%d" % (r, k, h) for k in range(l) for h in range(2)]
+            if r == RO - 1:
+                if l == 0:
+                    op("sv0", "storev", "Y", "dma", 262144, inp, (0,))
+                op("sv%d" % (l + 1), "storev", "Y", "dma", 262144, both, (l + 1,))
+            for k, n, m in ((0, 384, 1), (1, 384, 2), (2, 256, 2)):
+                op("vo%s%d" % (rl, k), "vote", "V", "tg", n, low + both[:m] + ["cp%s%d" % (rl, h) for h in range(m)] + [lst("cd", l)], (r, l, k))
+            op("h1_" + rl, "hop1", "G", "hop", 65536, ["vo%s0" % rl, "vo%s1" % rl], (r, l))
+            op("ex" + rl, "expand", "P", "pe", 6 * Q, ["g1_%d" % l, "m1", "m2", "mb", "vo%s2" % rl], (r, l), late=["h1_" + rl], reader="re" + rl)
+            op("re" + rl, "relu", "VS", "c1", Q, ["ex" + rl, "bias"], (r, l))
+            op("h2_" + rl, "hop2", "G", "hop", 65536, ["re" + rl], (r, l))
+            tab = ["irt%d" % r] + ["h2_%d%d" % (r, k) for k in range(l + 1)] + ["re%d%d" % (r, k) for k in range(l + 1)]
+            got, x = "re" + rl, ("ctp" if r == 0 else "wc%d%d3" % (r - 1, l))
+            for s in range(4):
+                tag = "%s%d" % (rl, s)
+                if not (r == 0 and l < 3 and s == 0):
+                    op("wg" + tag, "wgather", "VS", "g", Q, tab + [x], (r, l, s))
+                    got = "wg" + tag
+                if r == RO - 1 and l < 3 and s == 3:
+                    x = got
+                    break
+                op("wp" + tag, "wpe", "P", "pe", 16 * 64, [got, "zw"], (r, l, s), reader="wc" + tag)
+                op("wc" + tag, "wconv", "VS" if (r == RO - 1 and s == 3) else "V", "c1", 64, ["wp" + tag], (r, l, s))
+                x = "wc" + tag
+            if not (r == 1 and l == 3):
+                op("h3_" + rl, "hop3", "G", "hop", 65536 if (r == RO - 1 and l < 3) else 4096, [x], (r, l))
+            if r == 0 or l == L - 1:
+                src = src + both
+            else:
+                for h in range(2):
+                    op("u%s%d" % (rl, h), "u", "VS", "g", 512,
+                       low + both[:h + 1] + ["h3_%d%d" % (r - 1, l), "wc%d%d3" % (r - 1, l)], (r, l, h))
+                src = ["iu%d" % r] + ["u%d%d%d" % (r, k, h) for k in range(l + 1) for h in range(2)]
+        if r < RO - 1:
+            allv = inp + ["A%d%d%d" % (r, k, h) for k in range(L) for h in range(2)]
+            for h in range(2):
+                op("np%d_%d" % (r, h), "np", "VS", "g", 512, allv + (["ctp"] if r == 0 else ["h3_03", "wc033"]), (r, h))
+    op("syt", "storet", "Y", "dma", 32768, ["h3_23", "wc233"], ())
+    for t in ("fa", "fb"):
+        op("y0" + t, "y0", "V", "c1", 64, ["l%s0" % t], (t,))
+        for l in range(1, L):
+            tab = ["ir3"] + ["h3_2%d" % k for k in range(l)] + ["wg2%d3" % k for k in range(l)]
+            for h in range(2):
+                op("fg%s%d%d" % (t, l, h), "fgather", "VS", "g", 512, tab + [lst(t, l)], (t, l, h))
+            op("fp%s%d" % (t, l), "fpe", "P", "pe", 16 * 64, ["fg%s%d0" % (t, l), "fg%s%d1" % (t, l), "zw"], (t, l),
+               reader="fc%s%d" % (t, l))
+            op("fc%s%d" % (t, l), "fcopy", "VS", "c1", 64, ["fp%s%d" % (t, l)], (t, l))
+        op("sy%s0" % t, "storey", "Y", "dma", 98304, ["y0" + t, "fc%s1" % t, "fc%s2" % t], (t, 0, 192))
+        op("sy%s1" % t, "storey", "YS", "dma", 32768, ["fc%s3" % t], (t, 192, 256))
+    return ops
+
+
+OPS = build_ops()
+SEMAPHORES = ["cV", "cS", "cP", "cG", "sent"] + ["s_" + n for n, o in OPS.items() if o["cost"] in ("dma", "hop", "cp")]
+
+ORDER = """
+iip lx lfb0.S ixx lfa0.Y ipm lcd0.S lfb1.Y lfa1.Y lcd1.Y oh ipf iyy ltp.Y d0 kc m1c d64.S m1 d128.S dc d256.S md w1 m2 d512.S tg mb wc
+db4.S irt0 db1.V bias zw cfb0 y0fb B000.S cfa0 y0fa cfb1 B001.S A000 A001 cp000.S cfa1 B010.S cp001.G ccd0 vo000 B011.S A010 db2.S vo001
+cp010.Y A011 h1_00 g1_0.S vo002 B021.S cp011.G ccd1 ctp B020.S A021 A020 cp021.S vo010 ex00 B031.S cp020.G irt1 vo011 B030.S A031 h1_01
+re00.S vo020 db3.S wp000 h2_00 A030 g1_1.S vo021 np0_0.S vo012 h1_02 np0_1.S g1_2.V ex01 vo022 cp030.S iu1 wc000 cp031.V re01.S vo030
+B100.S wp010 h2_01 wg001.V B101.S vo031 wp001 wc010 ex02 h1_03 wc001 A100 wg002.S wp002 re02.S vo032 cp100.S h2_02 wp020 wc002 g1_3.S
+wg003.V A101 wp003 wg011.S wp011 wc020 cp101.S wc003 vo100 h3_00 ex03 wc011 vo101 wg012.S re03.S vo102 wp012 h1_10 wg021.V h2_03 wc012
+wp021 wg013.S wp013 wc021 u101.V wg022.S u100.S wp022 wc013 h3_01 wc022 B111.S wg023.V ex10 B110.V wp023 re10.S A110 h2_10 wg030.S wc023
+wp030 cp110.S A111 h3_02 cp111.V u111.S vo112 u110.S wc030 vo111 vo110 wg031.S B121.S B120.V wp031 h1_11 wg100.S A120 wp100 wc031 u120.S
+cp120.G irt2 A121 ir3 wg032.S cp121.V u121.S vo121 wp032 vo120 ex11 B131.S wc100 h1_12 wc032 re11.V wg033.S A131 h2_11 wg101.S wp033
+B130.S wp101 wc033 vo122 h3_03 cp131.S wc101 wg102.V A130 wp102 ex12 wc102 cp130.V wg103.S vo131 wp103 re12.S vo130 wg110.S h2_12 np1_0.S
+wp110 wc103 vo132 h3_10 np1_1.S wc110 wg111.V h1_13 wp111 B200.S iu2 sv0 wc111 B201.S A200 wg112.S A201 cp200.G u200.S wp112 wg120.V sv1
+u201.S wc112 cp201.G wp120 wg113.V wp113 wc120 vo200 wg121.S B211.S wc113 wp121 vo202 h3_11 vo201 ex13 B210.S wc121 h1_20 A211 wg122.S
+re13.S A210 wp122 cp211.G wc122 cp210.S sv2 wg123.V h2_13 u210.S wp123 vo212 vo210 u211.S ex20 wc123 vo211 h3_12 B221.S h1_21 re20.V
+B220.S A221 h2_20 A220 cp221.S wg130.S cp220.V sv3 u220.S wp130 vo220 u221.S vo221 ex21 vo222 h1_22 B230.S B231.V re21.S A230 wg200.S
+h2_21 wp200 A231 cp230.S vo230 cp231.S sv4 wc200 ex22 vo231 wg201.S wc130 h1_23 vo232 wp201 re22.S wg131.V h2_22 wc201 wp131 wg210.S
+wg202.S wp210 wc131 wg132.S wp202 wc210 wg211.V wp132 wc202 wg203.S ex23 wc132 wg133.S h3_20 wp211 re23.V h2_23 wg220.S wc211 wg212.V
+wp220 wp212 wc220 wg221.S wc212 wp221 wg213.S wp133 h3_21 wc221 fgfb11.S wg222.V wc133 wp222 fgfa10.S wg230.V wc222 wp230 fgfa11.S
+wg223.V h3_22 wc230 wg231.V fgfb10.V wp231 fpfa1 fgfa21.S wc231 wg232.V fgfb21.V fgfa20.S wp232 fpfb1 wc232 fgfb20.S wg233.V fcfb1.V
+wp233 fgfb31.V fcfa1.S fpfb2 wc233.S fgfa31.S fgfb30.V h3_23 fpfa2 fcfb2.S fgfa30.S fpfb3 syfb0 fcfa2.V syfa0 fcfb3.V fpfa3 syfb1.Y
+fcfa3.V syfa1.Y syt
+"""
+
+
+def finish_plan(order, eng):
+    pos = {n: i for i, n in enumerate(order)}
+    jobs = [n for n in order if OPS[n]["reader"]]
+    bank, extra = {}, {}
+    for j, n in enumerate(jobs):
+        bank[n] = bank[OPS[n]["reader"]] = j % 8
+        if j >= 8:
+            extra[n] = OPS[jobs[j - 8]]["reader"]
+    for n in order:
+        for d in OPS[n]["deps"] + OPS[n]["late"] + ([extra[n]] if n in extra else []):
+            if pos[d] > pos[n]:
+                return None
+    return order, eng, bank, extra
+
+
+def get_plan():
+    words = ORDER.split()
+    order = [w.split(".")[0] for w in words]
+    assert sorted(order) == sorted(OPS)
+    return finish_plan(order, {n: (w.split(".")[1] if "." in w else OPS[n]["eng"]) for n, w in zip(order, words)})
+
+
+def engine_masks(topo, cores, src):
+    far = [c for c in cores if topo.chip(c) != topo.chip(src)]
+    near = [c for c in cores if c != src and topo.chip(c) == topo.chip(src)]
+    out, used = {}, set()
+    for group in (far, near):
+        for i, c in enumerate(group):
+            es = [e for e in topo.engines(src, c) if e not in used]
+            k = len(es) // len(group)
+            out[c] = es[i * k:(i + 1) * k]
+        used |= set(e for c in group for e in out[c])
+    return out
+
+
+def rank_program(g, core, T, topo):
+    q = T.rank_of(core)
+    if q is None:
+        return
+    order, eng, bank, extra = get_plan()
+    cores = [int(c) for c in T.cores]
+    masks = {c: engine_masks(topo, cores, c) for c in cores}
+    arrive = sum(len(masks[c][core]) for c in cores if c != core)
+    leave = sum(len(v) for v in masks[core].values())
+    queue = {"V": g.vector, "S": g.scalar, "P": g.tensor, "G": g, "Y": g.sync}
+    A, F = AluOpType, ActivationFunctionType
+    count = {e: 0 for e in "VSPG"}
+    mark = {}
+    seen = {e: {} for e in queue}
+    sent = [0]
+
+    def wait(e, names):
+        need = {}
+        for a in names:
+            s, k = mark[a]
+            need[s] = max(need.get(s, 0), k)
+        for s, k in need.items():
+            if seen[e].get(s, 0) < k:
+                queue[e].wait_ge(T.sem[s], k)
+                seen[e][s] = k
+
+    def move(e, out, src):
+        if e == "V": return g.vector.tensor_copy(out, src)
+        if e == "S": return g.scalar.activation(out, src, F.Copy)
+        if e == "G": return g.affine_select(out, src, [[0, 512]], A.is_ge, 0.0, 0, 0)
+        return g.sync.dma_start(out, src)
+
+    def spread(name, pairs):
+        tr = []
+        for p in range(N):
+            if p == q: continue
+            rid, pid, se = topo.addr(cores[p])
+            m = sum(1 << e for e in masks[core][cores[p]])
+            tr.append(RemoteDMATransfer(dst_ids=[DstId(rid=rid, pnc=pid)], dma_engine_mask=m, remote_sem=T.sem["s_" + name],
+                                        src=pairs(p)[0], dst=pairs(p)[1]))
+        g.remote_dma_fused(tr, local_sem=T.sem.sent)
+        sent[0] += leave
+
+    def compact(ps, buf, a, n):
+        for i in range(16):
+            ins = g.tensor.matmul(ps[:, 0:n], T.zw[:, 15 - i:143 - i], buf[:, a + i:a + 16 * n:16], i == 0, i == 15)
+        return ins
+
+    col = lambda t, j: t[:, j:j + 1]
+    e0, e1, e2, e3 = [col(T.oh, j) for j in range(4)]
+    cc = {k: col(T.cc, j) for j, k in enumerate(("tg", "m1c", "dc", "bias", "w1", "wc"))}
+    pf = col(T.pf, 0)
+    own = lambda l: P + G * l + Q * q
+    slot = lambda r, l, s: (r * 4 + l) * 4 + s
+    xw = lambda r, l, s: T.xw[:, 16 * slot(r, l, s):16 * slot(r, l, s) + 16]
+
+    for name in order:
+        o, e = OPS[name], eng[name]
+        kind, a = o["kind"], o["args"]
+        wait(e, o["deps"] + ([extra[name]] if name in extra else []))
+        ps = T["ps%d" % bank[name]] if name in bank else None
+        ins = None
+        if kind == "load":
+            ins = queue[e].dma_start((T.v0 if a[0] == "x" else T[a[0] + "32"])[:, a[1]:a[2]], T[a[0]][:, a[1]:a[2]])
+        elif kind == "conv":
+            ins = g.vector.tensor_copy(T[a[0] + "16"][:, a[1]:a[2]], T[a[0] + "32"][:, a[1]:a[2]])
+        elif kind == "iota":
+            if a[0] == "ip": ins = g.iota(T.ip[:, 0:4], [[-1, 4]], 16, 1)
+            elif a[0] == "pf": ins = g.iota(pf, [[0, 1]], 0, 1, allow_small_or_imprecise_dtypes=True)
+            elif a[0] == "xx": ins = g.iota(T.xx[:, 0:146], [[1, 146]], -15, 0, allow_small_or_imprecise_dtypes=True)
+            else: ins = g.iota(T.yy[:], [[16, 8], [2, 8], [0, 2]], 0, 0, allow_small_or_imprecise_dtypes=True)
+        elif kind == "tiny":
+            t, ts = a[0], g.vector.tensor_scalar
+            if t == "ipm": ins = ts(T.ipm[:, 0:4], T.ip[:, 0:4], 15, None, A.bitwise_and)
+            elif t == "oh": ins = ts(T.oh[:, 0:4], T.ipm[:, 0:4], 0.0, None, A.is_equal)
+            elif t == "tg": ins = ts(cc["tg"], T.ipm[:, 0:1], -1.0, pf, A.mult, A.add)
+            elif t == "d0": ins = ts(T.dg[:, 0:64], T.xx[:, 15:79], e3, None, A.mult)
+            elif t == "kc": ins = ts(T.kc[:], T.xx[:, 15:95], e2, None, A.mult)
+            elif t == "m1c": ins = ts(cc["m1c"], e3, e2, None, A.subtract)
+            elif t == "dc": ins = ts(cc["dc"], e3, e2, None, A.add)
+            elif t == "bias": ins = ts(cc["bias"], e1, 64.0, e0, A.mult, A.add)
+            elif t == "w1": ins = ts(cc["w1"], e2, e0, 64.0, A.subtract, A.mult)
+            elif t == "wc": ins = ts(cc["wc"], cc["w1"], e1, e3, A.add, A.add)
+            elif t == "zw": ins = ts(T.zw[:, 0:143], T.xx[:, 0:143], cc["tg"], cc["wc"], A.is_equal, A.mult)
+            elif t == "m1": ins = ts(T.m1[:], T.xx[:, 17:145], pf, cc["m1c"], A.is_equal, A.mult)
+            elif t == "md": ins = ts(T.md[:], T.xx[:, 15:143], pf, cc["dc"], A.is_equal, A.mult)
+            elif t == "m2": ins = g.vector.tensor_tensor(T.m2[:], T.md[:], T.m1[:], A.subtract)
+            else: ins = ts(T.mb[:], T.yy[:], cc["tg"], -BIG, A.is_equal, A.mult)
+        elif kind == "dbl":
+            at, s0, n = a
+            out, src, b = T.dg[:, at:at + n], T.dg[:, s0:s0 + n], col(T.kc, at // 64)
+            if e == "V": ins = g.vector.tensor_scalar(out, src, b, None, A.add)
+            else: ins = g.scalar.activation(out, src, F.Identity, bias=b)
+        elif kind == "copyin":
+            ins = g.sync.dma_start(T[a[0]][:, 0:P], T.dg[:, 0:P])
+        elif kind == "g1":
+            l = a[0]
+            ins = move(e, T.g1[:, Q * l:Q * (l + 1)], T.dg[:, 0:P + G * (l + 1)].indirect(T.cd16[:, 64 * l + 16 * q:64 * l + 16 * q + 16]))
+        elif kind == "copyu":
+            ins = g.sync.dma_start(T["u%d" % a[0]][:, 0:P], T["v%d" % a[0]][:, 0:P])
+        elif kind in ("B", "A", "shadow"):
+            r, l, h = a
+            tab = T["v%d" % r] if (r == 0 or l == 0) else T["u%d" % r]
+            c0, at = 64 * l + 32 * h, P + G * l + 512 * h
+            nb = T.nb[:, (r * 4 + l) * G + 512 * h:(r * 4 + l) * G + 512 * (h + 1)]
+            if kind == "B":
+                win = tab[:, 0:P + G * l].indirect(T.fb16[:, c0:c0 + 32])
+                if e == "V": ins = g.vector.tensor_scalar(nb, win, -1.0, 255.0, A.mult, A.add)
+                else: ins = g.scalar.activation(nb, win, F.Identity, bias=255.0, scale=-1.0)
+            elif kind == "A":
+                ins = g.vector.tensor_tensor(T["v%d" % r][:, at:at + 512], tab[:, 0:P + G * l].indirect(T.fa16[:, c0:c0 + 32]), nb, A.min)
+            else:
+                ins = move(e, nb, T["v%d" % r][:, at:at + 512])
+        elif kind == "storev":
+            ins = g.sync.dma_start(T.yv[:, G * a[0]:G * (a[0] + 1)], T.v2[:, G * a[0]:G * (a[0] + 1)])
+        elif kind == "vote":
+            r, l, k = a
+            mine = [p for p in range(2 * k, 2 * k + 2) if p != q] if k < 2 else [q]
+            at, n, d0, c0 = P + G * l + Q * mine[0], Q * len(mine), (r * 4 + l) * G + Q * mine[0], 64 * l + 16 * mine[0]
+            ins = g.vector.tensor_tensor(T.df[:, d0:d0 + n], T["v%d" % r][:, 0:at + n].indirect(T.cd16[:, c0:c0 + n // 16]),
+                                         T.nb[:, d0:d0 + n], A.not_equal)
+        elif kind == "hop1":
+            r, l = a
+            d0 = (r * 4 + l) * G
+            land = lambda p: ((r * 4 + l) * 3 + (q - p - 1) % N) * Q
+            spread(name, lambda p: (T.df[:, d0 + Q * p:d0 + Q * (p + 1)], T.ld[:, land(p):land(p) + Q]))
+        elif kind == "expand":
+            r, l = a
+            d0 = (r * 4 + l) * G + Q * q
+            g.tensor.matmul(ps[:, 0:Q], T.m1[:], T.g1[:, Q * l:Q * (l + 1)], True, False)
+            g.tensor.matmul(ps[:, 0:Q], T.m2[:], T.dg[:, own(l):own(l) + Q], False, False)
+            g.tensor.matmul(ps[:, 0:Q], T.mb[:], T.df[:, d0:d0 + Q], False, False)
+            wait(e, o["late"])
+            for j in range(3):
+                j0 = ((r * 4 + l) * 3 + j) * Q
+                ins = g.tensor.matmul(ps[:, 0:Q], T.mb[:], T.ld[:, j0:j0 + Q], False, j == 2)
+        elif kind == "relu":
+            r, l = a
+            out = T["rt%d" % r][:, own(l):own(l) + Q]
+            if e == "V": ins = g.vector.tensor_scalar(out, ps[:, 0:Q], cc["bias"], 0.0, A.add, A.max)
+            else: ins = g.scalar.activation(out, ps[:, 0:Q], F.Relu, bias=cc["bias"])
+        elif kind == "hop2":
+            part = T["rt%d" % a[0]][:, own(a[1]):own(a[1]) + Q]
+            spread(name, lambda p: (part, part))
+        elif kind == "wgather":
+            r, l, s = a
+            c0 = 64 * l + 16 * q
+            if s > 0: x = xw(r, l, s - 1)
+            elif r == 0: x = T.tp16[:, 16 * q:16 * q + 16]
+            else: x = T["xl%d" % (r - 1)][:, c0:c0 + 16]
+            if r == RO - 1 and l < 3 and s == 3: out = T.r3[:, own(l):own(l) + Q]
+            else: out = T.gw[:, Q * slot(r, l, s):Q * slot(r, l, s) + Q]
+            ins = move(e, out, T["rt%d" % r][:, 0:P + G * (l + 1)].indirect(x))
+        elif kind == "wpe":
+            r, l, s = a
+            if r == 0 and l < 3 and s == 0: ins = compact(ps, T.rt0, own(l), 16)
+            else: ins = compact(ps, T.gw, Q * slot(r, l, s), 16)
+        elif kind == "wconv":
+            r, l, s = a
+            c0 = 64 * l + 16 * q
+            if s < 3: out = xw(r, l, s)
+            elif r < RO - 1: out = T["xl%d" % r][:, c0:c0 + 16]
+            else: out = T.yts[:, 16 * q:16 * q + 16]
+            ins = move(e, out, ps[:, 0:16])
+        elif kind == "hop3":
+            r, l = a
+            c0 = 64 * l + 16 * q
+            if r < RO - 1: part = T["xl%d" % r][:, c0:c0 + 16]
+            elif l < 3: part = T.r3[:, own(l):own(l) + Q]
+            else: part = T.yts[:, 16 * q:16 * q + 16]
+            spread(name, lambda p: (part, part))
+        elif kind == "u":
+            r, l, h = a
+            at, c0 = P + G * l + 512 * h, 64 * l + 32 * h
+            ins = move(e, T["u%d" % r][:, at:at + 512], T["v%d" % r][:, 0:at + 512].indirect(T["xl%d" % (r - 1)][:, c0:c0 + 32]))
+        elif kind == "np":
+            r, h = a
+            x = T.tp16[:, 32 * h:32 * h + 32] if r == 0 else T.xl0[:, 192 + 32 * h:224 + 32 * h]
+            ins = move(e, T["v%d" % (r + 1)][:, 512 * h:512 * h + 512], T["v%d" % r][:, 0:W].indirect(x))
+        elif kind == "storet":
+            ins = g.sync.dma_start(T.yt[:], T.yts[:])
+        elif kind == "y0":
+            ins = g.vector.tensor_copy(T["y%ss" % a[0][1]][:, 0:64], T[a[0] + "32"][:, 0:64])
+        elif kind == "fgather":
+            t, l, h = a
+            at, c0 = ((l - 1) * 2 + (t == "fb")) * G + 512 * h, 64 * l + 32 * h
+            ins = move(e, T.gf[:, at:at + 512], T.r3[:, 0:P + G * l].indirect(T[t + "16"][:, c0:c0 + 32]))
+        elif kind == "fpe":
+            t, l = a
+            ins = compact(ps, T.gf, ((l - 1) * 2 + (t == "fb")) * G, 64)
+        elif kind == "fcopy":
+            t, l = a
+            ins = move(e, T["y%ss" % t[1]][:, 64 * l:64 * l + 64], ps[:, 0:64])
+        elif kind == "storey":
+            t, c0, c1 = a
+            ins = queue[e].dma_start(T["y" + t[1]][:, c0:c1], T["y%ss" % t[1]][:, c0:c1])
+        if o["cost"] == "dma" or e == "Y":
+            ins.then_inc(T.sem["s_" + name], 16)
+            mark[name] = ("s_" + name, 16)
+        elif o["cost"] == "hop":
+            mark[name] = ("s_" + name, arrive)
+        else:
+            ins.then_inc(T.sem["c" + e], 1)
+            count[e] += 1
+            mark[name] = ("c" + e, count[e])
+    mark["sent"] = ("sent", sent[0])
+    wait("G", list(mark))

@@ -1,19 +1,22 @@
+import math
 from concourse.bass import DstId, RemoteDMATransfer
 from concourse.mybir import AluOpType, ActivationFunctionType
 
 N, P, L, G, RO = 4, 1024, 4, 1024, 3
 W = P + L * G
 Q = G // N
-BIG = 128.0
+H = G // 2
+BIG = 128
 
 SCRATCH = {}
 for _names, _cols, _dt in (
-        ("v0 v1 v2 rt0 rt1 rt2 dg", W, "bfloat16"), ("u1 u2 r3", 4096, "bfloat16"), ("nb df gw", 12 * G, "bfloat16"),
-        ("ld", 36 * Q, "bfloat16"), ("g1", G, "bfloat16"), ("gf", 6 * G, "bfloat16"), ("zw", 144, "bfloat16"),
-        ("m1 m2 md mb", 128, "bfloat16"), ("fa32 fb32 cd32", 256, "int32"), ("tp32", 64, "int32"), ("ip ipm", 8, "int32"),
-        ("fa16 fb16 cd16 xl0 xl1", 256, "uint16"), ("tp16", 64, "uint16"), ("xw", 48 * 16, "uint16"),
-        ("yas ybs", 256, "float32"), ("yts", 64, "float32"), ("oh pf cc", 8, "float32"), ("xx", 160, "float32"),
-        ("yy", 128, "float32"), ("kc", 80, "float32")):
+        ("v0 v1 v2 tb0 tb1 tb2 t1 t4", W, "bfloat16"), ("u1 u2 tb3", 4096, "bfloat16"), ("df gp", 12 * G, "bfloat16"),
+        ("gs gq gr", 12 * Q, "bfloat16"), ("gf", 6 * G, "bfloat16"), ("cnt", 12 * 4 * 64, "bfloat16"), ("dn", 12 * 64, "bfloat16"),
+        ("nd", 640, "bfloat16"), ("jt", 512, "bfloat16"), ("bk", G, "bfloat16"), ("one neg zs zw1 zw4 zq dm", 144, "bfloat16"),
+        ("fm", 160, "bfloat16"), ("eye jb", 128, "bfloat16"), ("b16", 16, "bfloat16"), ("fa32 fb32 cd32", 256, "int32"),
+        ("tp32 nn n2 jd", 64, "int32"), ("ja", 128, "int32"), ("ip ib", 8, "int32"), ("fa16 fb16 cd16 xl0 xl1", 256, "uint16"),
+        ("tp16", 64, "uint16"), ("xs", 128, "uint16"), ("xw", 12 * 64, "uint16"), ("yas ybs", 256, "float32"),
+        ("yts xx", 64, "float32"), ("cc kc gm wt", 16, "float32")):
     for _n in _names.split():
         SCRATCH[_n] = ("sbuf", [128, _cols], _dt)
 for _b in range(8):
@@ -23,153 +26,276 @@ for _b in range(8):
 def build_ops():
     ops = {}
 
-    def op(name, kind, eng, cost, n, deps, args=(), late=(), reader=None):
-        for d in list(deps) + list(late):
+    def op(name, kind, eng, cost, n, deps, args=(), bank=None):
+        for d in deps:
             assert d in ops, (name, d)
-        ops[name] = dict(name=name, kind=kind, eng=eng, cost=cost, n=n, deps=list(deps), late=list(late), args=args, reader=reader)
+        ops[name] = dict(name=name, kind=kind, eng=eng, cost=cost, n=n, deps=list(deps), args=args, bank=bank)
 
-    op("lx", "load", "Y", "dma", 262144, [], ("x", 0, P))
-    op("ltp", "load", "YS", "dma", 32768, [], ("tp", 0, 64))
-    for t in ("fb", "fa", "cd"):
-        op("l%s0" % t, "load", "YS", "dma", 32768, [], (t, 0, 64))
-        op("l%s1" % t, "load", "YS", "dma", 98304, [], (t, 64, 256))
+    def job(names, kinds, sizes, deps, reader, args):
+        bank = (names[0], names[-1])
+        for k in range(len(names) - 1):
+            op(names[k], kinds[k], "P", "pe", sizes[k], deps[k] + names[k - 1:k] * (k > 0), args, bank)
+        op(names[-1], kinds[-1], reader, "c1", sizes[-1], [names[-2]] + deps[-1], args, bank)
+
+    op("lx", "load", "Y", "dma", 2048, [], ("x", 0, P))
+    for t in ("fb", "fa"):
+        op("l%s0" % t, "load", "YS", "dma", 256, [], (t, 0, 64))
+        op("l%s1" % t, "load", "YS", "dma", 768, [], (t, 64, 256))
         op("c%s0" % t, "conv", "V", "c1", 64, ["l%s0" % t], (t, 0, 64))
         op("c%s1" % t, "conv", "V", "c1", 192, ["l%s1" % t], (t, 64, 256))
+    op("lcd", "load", "YS", "dma", 1024, [], ("cd", 0, 256))
+    op("ccd0", "conv", "V", "c1", 64, ["lcd"], ("cd", 0, 64))
+    op("ccd1", "conv", "V", "c1", 192, ["lcd"], ("cd", 64, 256))
+    op("ltp", "load", "Y", "dma", 256, [], ("tp", 0, 64))
     op("ctp", "conv", "V", "c1", 64, ["ltp"], ("tp", 0, 64))
+    op("lfill", "fill", "Y", "dma", 2048, [])
     lst = lambda t, l: "c%s%d" % (t, min(l, 1))
-    op("iip", "iota", "G", "iota", 4, [], ("ip",))
-    op("ipf", "iota", "G", "iota", 1, [], ("pf",))
-    op("ixx", "iota", "G", "iota", 146, [], ("xx",))
-    op("iyy", "iota", "G", "iota", 128, [], ("yy",))
-    tiny = [("ipm", ["iip"]), ("oh", ["ipm"]), ("tg", ["ipm", "ipf"]), ("d0", ["oh", "ixx"]), ("kc", ["oh", "ixx"]),
-            ("m1c", ["oh"]), ("dc", ["oh"]), ("bias", ["oh"]), ("w1", ["oh"]), ("wc", ["w1"]),
-            ("zw", ["wc", "tg", "ixx"]), ("m1", ["m1c", "ipf", "ixx"]), ("md", ["dc", "ipf", "ixx"]), ("m2", ["m1", "md"]),
-            ("mb", ["tg", "iyy"])]
-    for t, d in tiny:
-        op(t, "tiny", "V", "c1", {"zw": 143, "m1": 128, "md": 128, "m2": 256, "mb": 128, "kc": 80}.get(t, 64), d, (t,))
-    prev = "d0"
-    for s in (64, 128, 256, 512):
-        op("d%d" % s, "dbl", "VS", "ch", s, [prev, "kc"], (s, 0, s))
-        prev = "d%d" % s
-    for b in range(1, 5):
-        op("db%d" % b, "dbl", "VS", "ch", G, ["d512"], (G * b, 0, G))
-    op("irt0", "copyin", "Y", "dma", 262144, ["d512"], ("rt0",))
+    for t, n, d in (("ip", 1, []), ("xx", 64, []), ("nn", 64, []), ("one", 144, []), ("zs0", 144, ["one"]), ("zs", 144, ["zs0"]),
+                    ("eye", 128, ["one"]), ("dm", 136, ["one"]), ("neg", 144, []), ("fm0", 144, ["neg"]), ("fm", 144, ["fm0"]),
+                    ("zq", 144, [])):
+        op(t, "pool", "G", "pool", n, d, (t,))
+    for t, n, d in (("ib", 1, ["ip"]), ("i8", 1, ["ip"]), ("bf", 2, ["ib", "i8"]), ("al", 1, ["ib"]), ("be", 1, ["ib"]),
+                    ("ga", 1, ["ib", "al"]), ("kc", 9, ["al", "xx"]), ("nd0", 64, ["be", "ga", "xx"]), ("b16", 16, ["bf", "xx"]),
+                    ("n2", 64, ["bf", "nn"]), ("ws", 1, ["al"]), ("w0", 1, ["i8"]), ("wk", 5, ["bf", "xx"]),
+                    ("wt", 5, ["ws", "w0", "wk"]), ("jd", 64, ["n2", "lcd"]), ("jh", 64, ["jd"]), ("jl", 64, ["jd"]),
+                    ("jb", 128, ["jh", "jl"])):
+        op(t, "tiny", "V", "c1", n, d, (t,))
+    op("gm", "tiny", "VS", "c1", 8, ["zs"], ("gm",))
+    for k in (1, 4):
+        op("zw%d" % k, "zw", "VS", "ch", 144, ["zs", "wt"], (k,))
+    for k in range(4):
+        op("zq%d" % k, "zq", "VS", "c1", 8, ["zq", "gm", "wt"], (k,))
+    for k, (at, n) in enumerate(((64, 64), (128, 128), (256, 256), (512, 128))):
+        op("nd%d" % (k + 1), "dbl", "VS", "ch", n, ["nd%d" % min(k, 2), "kc"], (at, n))
+    op("zero", "zero", "V", "ch", P, [])
     for l in range(L):
-        op("g1_%d" % l, "g1", "VS", "g", Q, [lst("cd", l)] + ["db%d" % b for b in range(1, l + 2)], (l,))
+        op("fz%d" % l, "fillz", "Y", "dma", 2048, ["zero"], (l,))
+    op("tn", "names", "Y", "dma", 1280, ["nd3", "nd4"] + ["fz%d" % l for l in range(L)])
+    for b in range(8):
+        op("bk%d" % b, "block", "VS", "ch", 128, ["jb", "gm"], (b,))
+    job(["turn", "jt"], ["turn", "turned"], [8 * 64, 128], [["bk%d" % b for b in range(8)] + ["b16"], []], "VS", ())
+    op("h0_", "hop0", "G", "hop", 256, ["jt"])
+    for l in range(L):
+        op("tj%d" % l, "jump", "Y", "dma", 256, ["jt", "h0_", "fz%d" % l], (l,))
+    op("it4", "ident", "Y", "dma", 2048, ["tn"], ("t4",))
+    op("it3", "ident", "Y", "dma", 2048, ["tn"], ("tb3",))
+    tab = ["tn"] + ["tj%d" % l for l in range(L)]
+    got = [["sg0%d" % l for l in range(L)], ["sg10", "sg11"], ["sg20", "sg21"]]
+    for s in range(3):
+        for k, n in enumerate(got[s]):
+            op(n, "sgather", "VS", "g", G // len(got[s]), tab[:k + 2] + [lst("cd", k)] if s == 0 else tab + ["sc%d" % (s - 1)], (s, k))
+        if s < 2: job(["sp%d" % s, "sc%d" % s], ["spe", "sconv"], [16 * 64, 64], [got[s] + ["zw1"], []], "V", (s,))
+    for l in range(L):
+        job(["st%d" % l, "sq%d" % l], ["stack", "stacked"], [4 * Q, Q], [["sc1", "sg2%d" % (l // 2), "eye", "dm"], []], "VS", (l,))
+        op("hs%d" % l, "hops", "G", "hop", 512, ["sq%d" % l], (l,))
 
     for r in range(RO):
         inp = ["lx"] if r == 0 else ["np%d_0" % (r - 1), "np%d_1" % (r - 1)]
         if r > 0:
-            op("iu%d" % r, "copyu", "Y", "dma", 262144, inp, (r,))
-            for t in ["rt%d" % r] + ["r3"] * (r == RO - 1):
-                op("i" + t, "copyin", "Y", "dma", 262144, ["d512", "A%d20" % (r - 1)], (t,))
+            op("iu%d" % r, "copyu", "Y", "dma", 2048, inp, (r,))
         src = list(inp)
         for l in range(L):
-            rl = "%d%d" % (r, l)
-            for h in range(2):
-                op("B%s%d" % (rl, h), "B", "VS", "g", 512, src + [lst("fb", l)], (r, l, h))
-                op("A%s%d" % (rl, h), "A", "V", "tg", 512, src + [lst("fa", l), "B%s%d" % (rl, h)], (r, l, h))
-                op("cp%s%d" % (rl, h), "shadow", "YVSG", "cp", 512, ["A%s%d" % (rl, h)], (r, l, h))
-            both = ["A%s0" % rl, "A%s1" % rl]
+            rl, a = "%d%d" % (r, l), (r, l)
             low = inp + ["A%d%d%d" % (r, k, h) for k in range(l) for h in range(2)]
+            both = ["A%s0" % rl, "A%s1" % rl]
+            for h in range(2):
+                op("B%s%d" % (rl, h), "B", "VS", "g", H, src + [lst("fb", l)], (r, l, h))
+                op("A%s%d" % (rl, h), "A", "V", "g", H, src + [lst("fa", l), "B%s%d" % (rl, h)], (r, l, h))
+                op("cp%s%d" % (rl, h), "shadow", "YGVS", "cp", H, ["A%s%d" % (rl, h)], (r, l, h))
+                op("vo%s%d" % (rl, h), "vote", "V", "g", H, low + both[:h + 1] + ["cp%s%d" % (rl, h), lst("cd", l)], (r, l, h))
             if r == RO - 1:
                 if l == 0:
-                    op("sv0", "storev", "Y", "dma", 262144, inp, (0,))
-                op("sv%d" % (l + 1), "storev", "Y", "dma", 262144, both, (l + 1,))
-            for k, n, m in ((0, 384, 1), (1, 384, 2), (2, 256, 2)):
-                op("vo%s%d" % (rl, k), "vote", "V", "tg", n, low + both[:m] + ["cp%s%d" % (rl, h) for h in range(m)] + [lst("cd", l)], (r, l, k))
-            op("h1_" + rl, "hop1", "G", "hop", 65536, ["vo%s0" % rl, "vo%s1" % rl], (r, l))
-            op("ex" + rl, "expand", "P", "pe", 6 * Q, ["g1_%d" % l, "m1", "m2", "mb", "vo%s2" % rl], (r, l), late=["h1_" + rl], reader="re" + rl)
-            op("re" + rl, "relu", "VS", "c1", Q, ["ex" + rl, "bias"], (r, l))
-            op("h2_" + rl, "hop2", "G", "hop", 65536, ["re" + rl], (r, l))
-            tab = ["irt%d" % r] + ["h2_%d%d" % (r, k) for k in range(l + 1)] + ["re%d%d" % (r, k) for k in range(l + 1)]
-            got, x = "re" + rl, ("ctp" if r == 0 else "wc%d%d3" % (r - 1, l))
-            for s in range(4):
-                tag = "%s%d" % (rl, s)
-                if not (r == 0 and l < 3 and s == 0):
-                    op("wg" + tag, "wgather", "VS", "g", Q, tab + [x], (r, l, s))
-                    got = "wg" + tag
-                if r == RO - 1 and l < 3 and s == 3:
-                    x = got
-                    break
-                op("wp" + tag, "wpe", "P", "pe", 16 * 64, [got, "zw"], (r, l, s), reader="wc" + tag)
-                op("wc" + tag, "wconv", "VS" if (r == RO - 1 and s == 3) else "V", "c1", 64, ["wp" + tag], (r, l, s))
-                x = "wc" + tag
+                    op("sv0", "storev", "Y", "dma", 2048, inp, (0,))
+                op("sv%d" % (l + 1), "storev", "Y", "dma", 2048, both, (l + 1,))
+            job(["su" + rl, "sw" + rl, "cn" + rl], ["sum0", "sum1", "count"], [8 * 64, 8 * 64, 64],
+                [["vo%s0" % rl, "zs"], ["vo%s1" % rl], []], "VS", a)
+            op("h1_" + rl, "hop1", "G", "hop", 128, ["cn" + rl], a)
+            job(["ex" + rl, "mi" + rl], ["total", "totalled"], [4 * 64, 64], [["cn" + rl, "h1_" + rl, "eye"], []], "VS", a)
+            op("tw" + rl, "table", "Y", "dma", 128, ["mi" + rl], a)
+            tab = ["lfill" if r == 0 else "sw%d0" % (r - 1)] + ["tw%d%d" % (r, k) for k in range(l + 1)]
+            if r == 0 and l < 3:
+                rows, look = "sq%d" % l, [(Q, lst("cd", l)), (Q, "sc0"), (Q, "sc1")]
+            else:
+                x0 = "ctp" if r == 0 else "pl%d%d" % (r - 1, l)
+                rows, look = "qg" + rl, [(H, "qc" + rl), (H, "qc" + rl)]
+                op(rows, "qgather", "VS", "g", Q, ["it4", x0] + [t + str(k) for k in range(l + 1) for t in ("sq", "hs")], a)
+                job(["qa" + rl, "qc" + rl], ["qpe", "qconv"], [4 * 64, 64], [[rows] + ["zq%d" % k for k in range(4)], []], "V", a)
+            for k, (n, x) in enumerate(look):
+                op("pg%s%d" % (rl, k), "pgather", "VS", "g", n, tab + [x], (r, l, k))
+            job(["pa" + rl, "pb" + rl, "pr" + rl], ["prows", "pflags", "prelu"], [Q, 4 * Q, Q],
+                [[rows, "eye"], ["pg%s%d" % (rl, k) for k in range(len(look))] + ["fm"], ["it3"] * (r == RO - 1 and l < 3)], "VS", a)
+            x = "pr" + rl
+            if r < RO - 1 or l == 3:
+                x = "pl" + rl
+                job(["pp" + rl, x], ["ppe", "pconv"], [16 * 64, 16], [["pr" + rl, "zw4"], []], "VS" if r == RO - 1 else "V", a)
             if not (r == 1 and l == 3):
-                op("h3_" + rl, "hop3", "G", "hop", 65536 if (r == RO - 1 and l < 3) else 4096, [x], (r, l))
+                op("h3_" + rl, "hop3", "G", "hop", 512 if (r == RO - 1 and l < 3) else 32, [x], a)
             if r == 0 or l == L - 1:
                 src = src + both
             else:
                 for h in range(2):
-                    op("u%s%d" % (rl, h), "u", "VS", "g", 512,
-                       low + both[:h + 1] + ["h3_%d%d" % (r - 1, l), "wc%d%d3" % (r - 1, l)], (r, l, h))
+                    op("u%s%d" % (rl, h), "u", "VS", "g", H,
+                       low + both[:h + 1] + ["h3_%d%d" % (r - 1, l), "pl%d%d" % (r - 1, l)], (r, l, h))
                 src = ["iu%d" % r] + ["u%d%d%d" % (r, k, h) for k in range(l + 1) for h in range(2)]
         if r < RO - 1:
             allv = inp + ["A%d%d%d" % (r, k, h) for k in range(L) for h in range(2)]
             for h in range(2):
-                op("np%d_%d" % (r, h), "np", "VS", "g", 512, allv + (["ctp"] if r == 0 else ["h3_03", "wc033"]), (r, h))
-    op("syt", "storet", "Y", "dma", 32768, ["h3_23", "wc233"], ())
+                op("np%d_%d" % (r, h), "np", "VS", "g", H, allv + (["ctp"] if r == 0 else ["h3_03", "pl03"]), (r, h))
+    op("syt", "storet", "Y", "dma", 256, ["h3_23", "pl23"])
     for t in ("fa", "fb"):
         op("y0" + t, "y0", "V", "c1", 64, ["l%s0" % t], (t,))
         for l in range(1, L):
-            tab = ["ir3"] + ["h3_2%d" % k for k in range(l)] + ["wg2%d3" % k for k in range(l)]
+            tab = ["it3"] + ["h3_2%d" % k for k in range(l)] + ["pr2%d" % k for k in range(l)]
             for h in range(2):
-                op("fg%s%d%d" % (t, l, h), "fgather", "VS", "g", 512, tab + [lst(t, l)], (t, l, h))
-            op("fp%s%d" % (t, l), "fpe", "P", "pe", 16 * 64, ["fg%s%d0" % (t, l), "fg%s%d1" % (t, l), "zw"], (t, l),
-               reader="fc%s%d" % (t, l))
-            op("fc%s%d" % (t, l), "fcopy", "VS", "c1", 64, ["fp%s%d" % (t, l)], (t, l))
-        op("sy%s0" % t, "storey", "Y", "dma", 98304, ["y0" + t, "fc%s1" % t, "fc%s2" % t], (t, 0, 192))
-        op("sy%s1" % t, "storey", "YS", "dma", 32768, ["fc%s3" % t], (t, 192, 256))
+                op("fg%s%d%d" % (t, l, h), "fgather", "VS", "g", H, tab + [lst(t, l)], (t, l, h))
+            job(["fp%s%d" % (t, l), "fc%s%d" % (t, l)], ["fpe", "fcopy"], [16 * 64, 64],
+                [["fg%s%d0" % (t, l), "fg%s%d1" % (t, l), "zw4"], []], "VS", (t, l))
+        op("sy%s0" % t, "storey", "Y", "dma", 768, ["y0" + t, "fc%s1" % t, "fc%s2" % t], (t, 0, 192))
+        op("sy%s1" % t, "storey", "YS", "dma", 256, ["fc%s3" % t], (t, 192, 256))
     return ops
 
 
 OPS = build_ops()
 SEMAPHORES = ["cV", "cS", "cP", "cG", "sent"] + ["s_" + n for n, o in OPS.items() if o["cost"] in ("dma", "hop", "cp")]
 
-ORDER = """
-iip lx lfb0.S ixx lfa0.Y ipm lcd0.S lfb1.Y lfa1.Y lcd1.Y oh ipf iyy ltp.Y d0 kc m1c d64.S m1 d128.S dc d256.S md w1 m2 d512.S tg mb wc
-db4.S irt0 db1.V bias zw cfb0 y0fb B000.S cfa0 y0fa cfb1 B001.S A000 A001 cp000.S cfa1 B010.S cp001.G ccd0 vo000 B011.S A010 db2.S vo001
-cp010.Y A011 h1_00 g1_0.S vo002 B021.S cp011.G ccd1 ctp B020.S A021 A020 cp021.S vo010 ex00 B031.S cp020.G irt1 vo011 B030.S A031 h1_01
-re00.S vo020 db3.S wp000 h2_00 A030 g1_1.S vo021 np0_0.S vo012 h1_02 np0_1.S g1_2.V ex01 vo022 cp030.S iu1 wc000 cp031.V re01.S vo030
-B100.S wp010 h2_01 wg001.V B101.S vo031 wp001 wc010 ex02 h1_03 wc001 A100 wg002.S wp002 re02.S vo032 cp100.S h2_02 wp020 wc002 g1_3.S
-wg003.V A101 wp003 wg011.S wp011 wc020 cp101.S wc003 vo100 h3_00 ex03 wc011 vo101 wg012.S re03.S vo102 wp012 h1_10 wg021.V h2_03 wc012
-wp021 wg013.S wp013 wc021 u101.V wg022.S u100.S wp022 wc013 h3_01 wc022 B111.S wg023.V ex10 B110.V wp023 re10.S A110 h2_10 wg030.S wc023
-wp030 cp110.S A111 h3_02 cp111.V u111.S vo112 u110.S wc030 vo111 vo110 wg031.S B121.S B120.V wp031 h1_11 wg100.S A120 wp100 wc031 u120.S
-cp120.G irt2 A121 ir3 wg032.S cp121.V u121.S vo121 wp032 vo120 ex11 B131.S wc100 h1_12 wc032 re11.V wg033.S A131 h2_11 wg101.S wp033
-B130.S wp101 wc033 vo122 h3_03 cp131.S wc101 wg102.V A130 wp102 ex12 wc102 cp130.V wg103.S vo131 wp103 re12.S vo130 wg110.S h2_12 np1_0.S
-wp110 wc103 vo132 h3_10 np1_1.S wc110 wg111.V h1_13 wp111 B200.S iu2 sv0 wc111 B201.S A200 wg112.S A201 cp200.G u200.S wp112 wg120.V sv1
-u201.S wc112 cp201.G wp120 wg113.V wp113 wc120 vo200 wg121.S B211.S wc113 wp121 vo202 h3_11 vo201 ex13 B210.S wc121 h1_20 A211 wg122.S
-re13.S A210 wp122 cp211.G wc122 cp210.S sv2 wg123.V h2_13 u210.S wp123 vo212 vo210 u211.S ex20 wc123 vo211 h3_12 B221.S h1_21 re20.V
-B220.S A221 h2_20 A220 cp221.S wg130.S cp220.V sv3 u220.S wp130 vo220 u221.S vo221 ex21 vo222 h1_22 B230.S B231.V re21.S A230 wg200.S
-h2_21 wp200 A231 cp230.S vo230 cp231.S sv4 wc200 ex22 vo231 wg201.S wc130 h1_23 vo232 wp201 re22.S wg131.V h2_22 wc201 wp131 wg210.S
-wg202.S wp210 wc131 wg132.S wp202 wc210 wg211.V wp132 wc202 wg203.S ex23 wc132 wg133.S h3_20 wp211 re23.V h2_23 wg220.S wc211 wg212.V
-wp220 wp212 wc220 wg221.S wc212 wp221 wg213.S wp133 h3_21 wc221 fgfb11.S wg222.V wc133 wp222 fgfa10.S wg230.V wc222 wp230 fgfa11.S
-wg223.V h3_22 wc230 wg231.V fgfb10.V wp231 fpfa1 fgfa21.S wc231 wg232.V fgfb21.V fgfa20.S wp232 fpfb1 wc232 fgfb20.S wg233.V fcfb1.V
-wp233 fgfb31.V fcfa1.S fpfb2 wc233.S fgfa31.S fgfb30.V h3_23 fpfa2 fcfb2.S fgfa30.S fpfb3 syfb0 fcfa2.V syfa0 fcfb3.V fpfa3 syfb1.Y
-fcfa3.V syfa1.Y syt
-"""
+GUESSES = [dict(zip("cycle gather pe call sem issue start rissue rstart row byte first".split(), v)) for v in (
+    (0.00104, 0.0012, 0.00056, 0.06, 0.1, 0.2, 1.0, 0.6, 1.0, 0.02, 0.00004, 2.0),
+    (0.0012, 0.0012, 0.00066, 0.07, 0.1, 0.3, 0.6, 0.9, 1.3, 0.015, 0.00004, 2.0),
+    (0.0009, 0.0015, 0.0005, 0.04, 0.1, 0.1, 1.5, 0.6, 1.0, 0.04, 0.00006, 1.0))]
+LEAN, SWEEPS, STEPS = 0.8, 6, 50000
 
 
-def finish_plan(order, eng):
-    pos = {n: i for i, n in enumerate(order)}
-    jobs = [n for n in order if OPS[n]["reader"]]
-    bank, extra = {}, {}
-    for j, n in enumerate(jobs):
-        bank[n] = bank[OPS[n]["reader"]] = j % 8
-        if j >= 8:
-            extra[n] = OPS[jobs[j - 8]]["reader"]
+def needs(o, e, m):
+    c, n = o["cost"], o["n"]
+    if c == "dma" or (c == "cp" and e == "Y"): return m["issue"], m["start"], 8 * (m["row"] + n * m["byte"] * (2 if c == "cp" else 1))
+    if c == "hop": return m["rissue"], m["rstart"], 32 * (m["row"] + n * m["byte"])
+    if c == "g": return m["call"] + n * m["gather"], 0, 0
+    if c == "pe": return n * m["pe"], 0, 0
+    if e == "G": return 0.16 + 2 * n * m["cycle"], 0, 0
+    return m["call"] + max(64, n // 2 if (c in ("ch", "cp") and e == "V") else n) * m["cycle"], 0, 0
+
+
+def sweep(rank, before, back):
+    busy = {e: [] for e in "VSPGYD"}
+    start, end, eng = {}, {}, {}
+    todo = sorted(OPS, key=lambda n: rank[n])
+    while todo:
+        n = next(x for x in todo if all(d in end for d in before[x]))
+        todo.remove(n)
+        best = None
+        for e in OPS[n]["eng"][:2]:
+            hold, off, d = needs(OPS[n], e, GUESSES[0])
+            t = off + d if d else hold
+            use = [(e, t - hold if back else 0.0, hold)] + [("D", 0.0 if back else off, d)] * (d > 0)
+            s, moved = max([end[x] + GUESSES[0]["sem"] for x in before[n]] + [0.0]), True
+            while moved:
+                moved = False
+                for res, o, w in use:
+                    for a, b in busy[res]:
+                        if a < s + o + w - 1e-9 and s + o < b - 1e-9: s, moved = b - o, True
+            key = s + t + (LEAN if e == "V" else 0.0)
+            if best is None or key < best[0]: best = (key, s, t, e, use)
+        key, s, t, e, use = best
+        for res, o, w in use:
+            busy[res].append((s + o, s + o + w))
+            busy[res].sort()
+        start[n], end[n], eng[n] = s, s + t, e
+    return start, end, eng
+
+
+def with_banks(order, eng):
+    free, bank, extra = [(b, None) for b in range(8)], {}, {}
     for n in order:
-        for d in OPS[n]["deps"] + OPS[n]["late"] + ([extra[n]] if n in extra else []):
-            if pos[d] > pos[n]:
-                return None
+        if OPS[n]["bank"]:
+            job, reader = OPS[n]["bank"]
+            if n == job:
+                if not free: return None
+                bank[job], last = free.pop(0)
+                if last: extra[n] = last
+            if n == reader: free.append((bank[job], n))
     return order, eng, bank, extra
 
 
-def get_plan():
-    words = ORDER.split()
-    order = [w.split(".")[0] for w in words]
-    assert sorted(order) == sorted(OPS)
-    return finish_plan(order, {n: (w.split(".")[1] if "." in w else OPS[n]["eng"]) for n, w in zip(order, words)})
+def replay(plan, deps, costs, m):
+    free, last, done, why = dict.fromkeys("VSPGY", 0.0), dict.fromkeys("VSPGYD"), {}, {}
+    dma, first, sem, extra, eng = 0.0, m["first"], m["sem"], plan[3], plan[1]
+    for n in plan[0]:
+        e = eng[n]
+        t, w, queued = free[e], last[e], True
+        for d in deps[n] + [extra[n]] if n in extra else deps[n]:
+            if done[d] + sem > t: t, w, queued = done[d] + sem, d, False
+        hold, off, d = costs[n, e]
+        if d and e == "G": t, first = t + first, 0.0
+        free[e] = done[n] = t + hold
+        if d:
+            if dma > t + off: w, queued = last["D"], True
+            dma = done[n] = max(dma, t + off) + d
+            last["D"] = n
+        last[e], why[n] = n, (w, queued)
+    end = max(done, key=done.get)
+    return done[end], end, why
+
+
+def make_plan():
+    before = {n: o["deps"] for n, o in OPS.items()}
+    after = {n: [x for x in OPS if n in before[x]] for n in OPS}
+    index = {n: i for i, n in enumerate(OPS)}
+    start, end, eng = sweep(index, before, False)
+    for k in range(SWEEPS):
+        start, end, eng = sweep({n: -end[n] for n in OPS}, after, True)
+        start, end, eng = sweep({n: -end[n] for n in OPS}, before, False)
+    below = {}
+    for n in OPS:
+        below[n] = set(before[n]).union(*[below[d] for d in before[n]])
+    deps = {n: [d for d in dict.fromkeys(before[n]) if not any(d in below[x] for x in before[n])] for n in OPS}
+    costs = [{(n, e): needs(o, e, m) for n, o in OPS.items() for e in o["eng"]} for m in GUESSES]
+    state = [12345]
+
+    def draw(k):
+        state[0] = (state[0] * 1103515245 + 12345) % 2 ** 31
+        return (state[0] >> 8) % k
+
+    def weigh(plan):
+        runs = [replay(plan, deps, c, m) for c, m in zip(costs, GUESSES)]
+        return sum(x[0] for x in runs) / len(runs), runs
+
+    plan = with_banks(sorted(OPS, key=lambda n: (start[n], index[n])), eng)
+    now, runs = weigh(plan)
+    best = (now, plan)
+    for step in range(STEPS):
+        total, n, why = runs[draw(len(runs))]
+        pairs = []
+        while n:
+            if why[n][0] and why[n][1]: pairs.append((why[n][0], n))
+            n = why[n][0]
+        a, b = pairs[draw(len(pairs))]
+        order, eng, how = plan[0], plan[1], draw(10)
+        if how < 3:
+            n = (a, b, order[draw(len(order))])[how]
+            eng = dict(eng)
+            eng[n] = OPS[n]["eng"][draw(len(OPS[n]["eng"]))]
+            if eng[n] == plan[1][n]: continue
+        else:
+            far = (0, 0, 4, 10, 25)[draw(5)]
+            i, j = order.index(a), order.index(b)
+            if how < 7: i, keep, links, part = max(0, i - far), {b}, deps, order[max(0, i - far):j + 1][::-1]
+            else: j, keep, links, part = j + far, {a}, after, order[i:j + far + 1]
+            for n in part:
+                if n in keep: keep.update(links[n])
+            if a in keep and b in keep: continue
+            part = order[i:j + 1]
+            order = order[:i] + sorted(part, key=lambda n: (n in keep) != (how < 7)) + order[j + 1:]
+        new = with_banks(order, eng)
+        if new is None: continue
+        total, tried = weigh(new)
+        heat = 0.06 * (0.2 ** (step / STEPS))
+        if total <= now or draw(10000) < 10000 * math.exp((now - total) / heat):
+            now, runs, plan = total, tried, new
+            if now < best[0]: best = (now, plan)
+    return best[1]
+
+
+PLAN = make_plan()
 
 
 def engine_masks(topo, cores, src):
@@ -189,7 +315,7 @@ def rank_program(g, core, T, topo):
     q = T.rank_of(core)
     if q is None:
         return
-    order, eng, bank, extra = get_plan()
+    order, eng, bank, extra = PLAN
     cores = [int(c) for c in T.cores]
     masks = {c: engine_masks(topo, cores, c) for c in cores}
     arrive = sum(len(masks[c][core]) for c in cores if c != core)
@@ -214,167 +340,213 @@ def rank_program(g, core, T, topo):
     def move(e, out, src):
         if e == "V": return g.vector.tensor_copy(out, src)
         if e == "S": return g.scalar.activation(out, src, F.Copy)
-        if e == "G": return g.affine_select(out, src, [[0, 512]], A.is_ge, 0.0, 0, 0)
+        if e == "G": return g.affine_select(out, src, [[0, H]], A.is_ge, 0.0, 0, 0)
         return g.sync.dma_start(out, src)
 
-    def spread(name, pairs):
+    def scaled(e, out, src, m):
+        if e == "V": return g.vector.tensor_scalar(out, src, m, None, A.mult)
+        return g.scalar.activation(out, src, F.Identity, scale=m)
+
+    def spread(name, part):
         tr = []
         for p in range(N):
             if p == q: continue
             rid, pid, se = topo.addr(cores[p])
             m = sum(1 << e for e in masks[core][cores[p]])
             tr.append(RemoteDMATransfer(dst_ids=[DstId(rid=rid, pnc=pid)], dma_engine_mask=m, remote_sem=T.sem["s_" + name],
-                                        src=pairs(p)[0], dst=pairs(p)[1]))
+                                        src=part, dst=part))
         g.remote_dma_fused(tr, local_sem=T.sem.sent)
         sent[0] += leave
 
-    def compact(ps, buf, a, n):
+    def compact(out, k, buf, a, n):
         for i in range(16):
-            ins = g.tensor.matmul(ps[:, 0:n], T.zw[:, 15 - i:143 - i], buf[:, a + i:a + 16 * n:16], i == 0, i == 15)
+            ins = g.tensor.matmul(out, T["zw%d" % k][:, 15 - i:143 - i], buf[:, a + i:a + 16 * n:16], i == 0, i == 15)
         return ins
 
     col = lambda t, j: t[:, j:j + 1]
-    e0, e1, e2, e3 = [col(T.oh, j) for j in range(4)]
-    cc = {k: col(T.cc, j) for j, k in enumerate(("tg", "m1c", "dc", "bias", "w1", "wc"))}
-    pf = col(T.pf, 0)
-    own = lambda l: P + G * l + Q * q
-    slot = lambda r, l, s: (r * 4 + l) * 4 + s
-    xw = lambda r, l, s: T.xw[:, 16 * slot(r, l, s):16 * slot(r, l, s) + 16]
+    cut = lambda t, k, n, m=1: t[:, k * n:(k + m) * n]
+    cc = {k: col(T.cc, j) for j, k in enumerate(("bf", "mf", "al", "be", "ga", "ws", "w0"))}
+    own = lambda t, l: t[:, P + G * l + Q * q:P + G * l + Q * q + Q]
+    mine = lambda t, l: t[:, 64 * l + 16 * q:64 * l + 16 * q + 16]
+    cnt = lambda r, l, p: cut(T.cnt, (r * 4 + l) * 4 + p, 64)
+    df = lambda r, l, a, b: T["tb%d" % (r + 1)][:, a:b] if (l == 0 and r < RO - 1) else T.df[:, (r * 4 + l) * G + a:(r * 4 + l) * G + b]
 
     for name in order:
         o, e = OPS[name], eng[name]
         kind, a = o["kind"], o["args"]
-        wait(e, o["deps"] + ([extra[name]] if name in extra else []))
-        ps = T["ps%d" % bank[name]] if name in bank else None
+        wait(e, [d for d in o["deps"] if not (e == "P" and OPS[d]["bank"] == o["bank"])] + ([extra[name]] if name in extra else []))
+        ps = T["ps%d" % bank[o["bank"][0]]] if o["bank"] else None
+        ts, ib = g.vector.tensor_scalar, col(T.ib, 0)
         ins = None
         if kind == "load":
             ins = queue[e].dma_start((T.v0 if a[0] == "x" else T[a[0] + "32"])[:, a[1]:a[2]], T[a[0]][:, a[1]:a[2]])
+        elif kind == "fill":
+            ins = g.sync.dma_start(T.tb0[:, 0:P], T.x[:])
         elif kind == "conv":
             ins = g.vector.tensor_copy(T[a[0] + "16"][:, a[1]:a[2]], T[a[0] + "32"][:, a[1]:a[2]])
-        elif kind == "iota":
-            if a[0] == "ip": ins = g.iota(T.ip[:, 0:4], [[-1, 4]], 16, 1)
-            elif a[0] == "pf": ins = g.iota(pf, [[0, 1]], 0, 1, allow_small_or_imprecise_dtypes=True)
-            elif a[0] == "xx": ins = g.iota(T.xx[:, 0:146], [[1, 146]], -15, 0, allow_small_or_imprecise_dtypes=True)
-            else: ins = g.iota(T.yy[:], [[16, 8], [2, 8], [0, 2]], 0, 0, allow_small_or_imprecise_dtypes=True)
+        elif kind == "pool":
+            t, small = a[0], dict(allow_small_or_imprecise_dtypes=True)
+            if t == "ip": ins = g.iota(col(T.ip, 0), [[0, 1]], 0, 1)
+            elif t == "xx": ins = g.iota(T.xx[:], [[1, 64]], 0, 0, **small)
+            elif t == "nn": ins = g.iota(T.nn[:], [[16, 64]], P + G * q, 0)
+            elif t in ("one", "neg", "zq"): ins = g.iota(T[t][:], [[0, 144]], {"one": 1, "neg": -BIG, "zq": 0}[t], 0, **small)
+            elif t == "zs0": ins = g.affine_select(T.zs[:], T.one[:], [[-16, 9], [1000, 16]], A.is_ge, 0.0, -15000, 1)
+            elif t == "zs": ins = g.affine_select(T.zs[:], T.zs[:], [[16, 9], [0, 16]], A.is_ge, 0.0, 15, -1)
+            elif t == "eye": ins = g.affine_select(T.eye[:], T.one[:, 0:128], [[-1, 128]], A.is_equal, 0.0, 0, 1)
+            elif t == "dm": ins = g.affine_select(T.dm[:, 0:136], T.one[:, 0:136], [[-8, 17], [1000, 8]], A.is_equal, 0.0, -4001, 1)
+            elif t == "fm0": ins = g.affine_select(T.fm[:, 1:145], T.neg[:], [[-16, 9], [0, 16]], A.is_equal, 0.0, 16, 1)
+            else: ins = g.affine_select(T.fm[:, 1:145], T.fm[:, 1:145], [[0, 18], [1, 2], [0, 4]], A.is_equal, 0.0, 0, 0)
         elif kind == "tiny":
-            t, ts = a[0], g.vector.tensor_scalar
-            if t == "ipm": ins = ts(T.ipm[:, 0:4], T.ip[:, 0:4], 15, None, A.bitwise_and)
-            elif t == "oh": ins = ts(T.oh[:, 0:4], T.ipm[:, 0:4], 0.0, None, A.is_equal)
-            elif t == "tg": ins = ts(cc["tg"], T.ipm[:, 0:1], -1.0, pf, A.mult, A.add)
-            elif t == "d0": ins = ts(T.dg[:, 0:64], T.xx[:, 15:79], e3, None, A.mult)
-            elif t == "kc": ins = ts(T.kc[:], T.xx[:, 15:95], e2, None, A.mult)
-            elif t == "m1c": ins = ts(cc["m1c"], e3, e2, None, A.subtract)
-            elif t == "dc": ins = ts(cc["dc"], e3, e2, None, A.add)
-            elif t == "bias": ins = ts(cc["bias"], e1, 64.0, e0, A.mult, A.add)
-            elif t == "w1": ins = ts(cc["w1"], e2, e0, 64.0, A.subtract, A.mult)
-            elif t == "wc": ins = ts(cc["wc"], cc["w1"], e1, e3, A.add, A.add)
-            elif t == "zw": ins = ts(T.zw[:, 0:143], T.xx[:, 0:143], cc["tg"], cc["wc"], A.is_equal, A.mult)
-            elif t == "m1": ins = ts(T.m1[:], T.xx[:, 17:145], pf, cc["m1c"], A.is_equal, A.mult)
-            elif t == "md": ins = ts(T.md[:], T.xx[:, 15:143], pf, cc["dc"], A.is_equal, A.mult)
-            elif t == "m2": ins = g.vector.tensor_tensor(T.m2[:], T.md[:], T.m1[:], A.subtract)
-            else: ins = ts(T.mb[:], T.yy[:], cc["tg"], -BIG, A.is_equal, A.mult)
+            t = a[0]
+            if t == "ib": ins = ts(ib, col(T.ip, 0), 15, None, A.bitwise_and)
+            elif t == "i8": ins = ts(col(T.ib, 1), col(T.ip, 0), 7, None, A.bitwise_and)
+            elif t == "bf": ins = g.vector.tensor_copy(T.cc[:, 0:2], T.ib[:, 0:2])
+            elif t == "al": ins = ts(cc["al"], ib, 8.0, None, A.is_lt)
+            elif t == "be": ins = ts(cc["be"], ib, 8.0, None, A.is_ge)
+            elif t == "ga": ins = ts(cc["ga"], ib, 10.0, cc["al"], A.mult, A.mult)
+            elif t == "kc": ins = ts(T.kc[:, 0:9], T.xx[:, 0:9], cc["al"], None, A.mult)
+            elif t == "nd0": ins = ts(T.nd[:, 0:64], T.xx[:, 0:64], cc["be"], cc["ga"], A.mult, A.add)
+            elif t == "b16": ins = ts(T.b16[:], T.xx[:, 0:16], cc["bf"], None, A.is_equal)
+            elif t == "n2": ins = ts(T.n2[:], T.nn[:], cc["bf"], None, A.add)
+            elif t == "ws": ins = ts(cc["ws"], cc["al"], 63.0, 1.0, A.mult, A.add)
+            elif t == "w0": ins = ts(cc["w0"], col(T.ib, 1), 0.0, 2.0, A.is_equal, A.mult)
+            elif t == "wk": ins = ts(T.wt[:, 8:13], T.xx[:, 0:5], cc["mf"], -1.0, A.is_ge, A.mult)
+            elif t == "wt": ins = ts(T.wt[:, 0:5], T.wt[:, 8:13], cc["w0"], cc["ws"], A.add, A.mult)
+            elif t == "jd": ins = g.vector.tensor_tensor(T.jd[:], T.n2[:], cut(T.cd32, q, 64), A.subtract)
+            elif t == "jh": ins = ts(T.ja[:, 0:64], T.jd[:], 6, None, A.arith_shift_right)
+            elif t == "jl": ins = ts(T.ja[:, 64:128], T.jd[:], 63, None, A.bitwise_and)
+            elif t == "jb": ins = g.vector.tensor_copy(T.jb[:], T.ja[:])
+            else: ins = move(e, T.gm[:, 0:8], T.zs[:, 15:128:16])
+        elif kind == "zw":
+            ins = scaled(e, T["zw%d" % a[0]][:], T.zs[:], col(T.wt, a[0]))
+        elif kind == "zq":
+            ins = scaled(e, T.zq[:, 4 * a[0] + 3:128:16], T.gm[:, 0:8], col(T.wt, a[0]))
         elif kind == "dbl":
-            at, s0, n = a
-            out, src, b = T.dg[:, at:at + n], T.dg[:, s0:s0 + n], col(T.kc, at // 64)
-            if e == "V": ins = g.vector.tensor_scalar(out, src, b, None, A.add)
+            at, n = a
+            out, src, b = T.nd[:, at:at + n], T.nd[:, 0:n], col(T.kc, at // 64)
+            if e == "V": ins = ts(out, src, b, None, A.add)
             else: ins = g.scalar.activation(out, src, F.Identity, bias=b)
-        elif kind == "copyin":
-            ins = g.sync.dma_start(T[a[0]][:, 0:P], T.dg[:, 0:P])
-        elif kind == "g1":
-            l = a[0]
-            ins = move(e, T.g1[:, Q * l:Q * (l + 1)], T.dg[:, 0:P + G * (l + 1)].indirect(T.cd16[:, 64 * l + 16 * q:64 * l + 16 * q + 16]))
+        elif kind == "zero":
+            ins = g.vector.memset(T.t1[:, 0:P], 0.0)
+        elif kind == "fillz":
+            ins = g.sync.dma_start(cut(T.t1, a[0] + 1, G), T.t1[:, 0:P])
+        elif kind == "names":
+            ins = g.sync.dma_start(T.t1[0:128:8, :], T.nd[:])
+        elif kind == "block":
+            ins = scaled(e, cut(T.bk, a[0], 128), T.jb[:], col(T.gm, a[0]))
+        elif kind == "turn":
+            for j in range(8):
+                ins = g.tensor.matmul(cut(ps, j, 16), T.bk[:, j:G:8], T.b16[:], True, True)
+        elif kind == "turned":
+            ins = move(e, cut(T.jt, q, 128), ps[:, 0:128])
+        elif kind == "hop0":
+            spread(name, cut(T.jt, q, 128))
+        elif kind == "jump":
+            ins = g.sync.dma_start(T.t1[1:128:8, P + G * a[0]:P + G * (a[0] + 1)], cut(T.jt, a[0], 128))
+        elif kind == "ident":
+            ins = g.sync.dma_start(T[a[0]][:, 0:P], T.t1[:, 0:P])
+        elif kind == "sgather":
+            s, k = a
+            if s == 0: ins = move(e, cut(T.gs, k, Q), T.t1[:, 0:P + G * (k + 1)].indirect(mine(T.cd16, k)))
+            else: ins = move(e, cut(T.gs, 2 * s + k, H), T.t1[:].indirect(cut(T.xs, 2 * s + k - 2, 32)))
+        elif kind == "spe":
+            ins = compact(ps[:, 0:64], 1, T.gs, a[0] * G, 64)
+        elif kind == "sconv":
+            ins = move(e, cut(T.xs, a[0], 64), ps[:, 0:64])
+        elif kind == "stack":
+            g.tensor.matmul(ps[:, 0:Q], T.eye[:], own(T.t1, a[0]), True, False)
+            for s in range(3):
+                ins = g.tensor.matmul(ps[:, 0:Q], T.dm[:, 2 - s:130 - s], cut(T.gs, 4 * s + a[0], Q), False, s == 2)
+        elif kind == "stacked":
+            ins = move(e, own(T.t4, a[0]), ps[:, 0:Q])
+        elif kind == "hops":
+            spread(name, own(T.t4, a[0]))
         elif kind == "copyu":
             ins = g.sync.dma_start(T["u%d" % a[0]][:, 0:P], T["v%d" % a[0]][:, 0:P])
-        elif kind in ("B", "A", "shadow"):
+        elif kind in ("B", "A", "shadow", "vote"):
             r, l, h = a
-            tab = T["v%d" % r] if (r == 0 or l == 0) else T["u%d" % r]
-            c0, at = 64 * l + 32 * h, P + G * l + 512 * h
-            nb = T.nb[:, (r * 4 + l) * G + 512 * h:(r * 4 + l) * G + 512 * (h + 1)]
+            v = T["v%d" % r]
+            tab = v if (r == 0 or l == 0) else T["u%d" % r]
+            c0, at = 64 * l + 32 * h, P + G * l + H * h
+            nb = T["tb%d" % r][:, at:at + H]
             if kind == "B":
                 win = tab[:, 0:P + G * l].indirect(T.fb16[:, c0:c0 + 32])
-                if e == "V": ins = g.vector.tensor_scalar(nb, win, -1.0, 255.0, A.mult, A.add)
+                if e == "V": ins = ts(nb, win, -1.0, 255.0, A.mult, A.add)
                 else: ins = g.scalar.activation(nb, win, F.Identity, bias=255.0, scale=-1.0)
             elif kind == "A":
-                ins = g.vector.tensor_tensor(T["v%d" % r][:, at:at + 512], tab[:, 0:P + G * l].indirect(T.fa16[:, c0:c0 + 32]), nb, A.min)
+                ins = g.vector.tensor_tensor(v[:, at:at + H], tab[:, 0:P + G * l].indirect(T.fa16[:, c0:c0 + 32]), nb, A.min)
+            elif kind == "shadow":
+                ins = move(e, nb, v[:, at:at + H])
             else:
-                ins = move(e, nb, T["v%d" % r][:, at:at + 512])
+                ins = g.vector.tensor_tensor(df(r, l, H * h, H * h + H), v[:, 0:at + H].indirect(T.cd16[:, c0:c0 + 32]), nb, A.not_equal)
+        elif kind in ("sum0", "sum1"):
+            for i in range(8 * int(kind[3]), 8 * int(kind[3]) + 8):
+                ins = g.tensor.matmul(ps[:, 0:64], T.zs[:, 15 - i:143 - i], df(a[0], a[1], 64 * i, 64 * i + 64), i == 0, i == 15)
         elif kind == "storev":
             ins = g.sync.dma_start(T.yv[:, G * a[0]:G * (a[0] + 1)], T.v2[:, G * a[0]:G * (a[0] + 1)])
-        elif kind == "vote":
-            r, l, k = a
-            mine = [p for p in range(2 * k, 2 * k + 2) if p != q] if k < 2 else [q]
-            at, n, d0, c0 = P + G * l + Q * mine[0], Q * len(mine), (r * 4 + l) * G + Q * mine[0], 64 * l + 16 * mine[0]
-            ins = g.vector.tensor_tensor(T.df[:, d0:d0 + n], T["v%d" % r][:, 0:at + n].indirect(T.cd16[:, c0:c0 + n // 16]),
-                                         T.nb[:, d0:d0 + n], A.not_equal)
+        elif kind == "count":
+            ins = move(e, cnt(a[0], a[1], q), ps[:, 0:64])
         elif kind == "hop1":
-            r, l = a
-            d0 = (r * 4 + l) * G
-            land = lambda p: ((r * 4 + l) * 3 + (q - p - 1) % N) * Q
-            spread(name, lambda p: (T.df[:, d0 + Q * p:d0 + Q * (p + 1)], T.ld[:, land(p):land(p) + Q]))
-        elif kind == "expand":
-            r, l = a
-            d0 = (r * 4 + l) * G + Q * q
-            g.tensor.matmul(ps[:, 0:Q], T.m1[:], T.g1[:, Q * l:Q * (l + 1)], True, False)
-            g.tensor.matmul(ps[:, 0:Q], T.m2[:], T.dg[:, own(l):own(l) + Q], False, False)
-            g.tensor.matmul(ps[:, 0:Q], T.mb[:], T.df[:, d0:d0 + Q], False, False)
-            wait(e, o["late"])
-            for j in range(3):
-                j0 = ((r * 4 + l) * 3 + j) * Q
-                ins = g.tensor.matmul(ps[:, 0:Q], T.mb[:], T.ld[:, j0:j0 + Q], False, j == 2)
-        elif kind == "relu":
-            r, l = a
-            out = T["rt%d" % r][:, own(l):own(l) + Q]
-            if e == "V": ins = g.vector.tensor_scalar(out, ps[:, 0:Q], cc["bias"], 0.0, A.add, A.max)
-            else: ins = g.scalar.activation(out, ps[:, 0:Q], F.Relu, bias=cc["bias"])
-        elif kind == "hop2":
-            part = T["rt%d" % a[0]][:, own(a[1]):own(a[1]) + Q]
-            spread(name, lambda p: (part, part))
-        elif kind == "wgather":
-            r, l, s = a
-            c0 = 64 * l + 16 * q
-            if s > 0: x = xw(r, l, s - 1)
-            elif r == 0: x = T.tp16[:, 16 * q:16 * q + 16]
-            else: x = T["xl%d" % (r - 1)][:, c0:c0 + 16]
-            if r == RO - 1 and l < 3 and s == 3: out = T.r3[:, own(l):own(l) + Q]
-            else: out = T.gw[:, Q * slot(r, l, s):Q * slot(r, l, s) + Q]
-            ins = move(e, out, T["rt%d" % r][:, 0:P + G * (l + 1)].indirect(x))
-        elif kind == "wpe":
-            r, l, s = a
-            if r == 0 and l < 3 and s == 0: ins = compact(ps, T.rt0, own(l), 16)
-            else: ins = compact(ps, T.gw, Q * slot(r, l, s), 16)
-        elif kind == "wconv":
-            r, l, s = a
-            c0 = 64 * l + 16 * q
-            if s < 3: out = xw(r, l, s)
-            elif r < RO - 1: out = T["xl%d" % r][:, c0:c0 + 16]
-            else: out = T.yts[:, 16 * q:16 * q + 16]
-            ins = move(e, out, ps[:, 0:16])
+            spread(name, cnt(a[0], a[1], q))
+        elif kind == "total":
+            for p in range(N):
+                ins = g.tensor.matmul(ps[:, 0:64], T.eye[:], cnt(a[0], a[1], p), p == 0, p == N - 1)
+        elif kind == "totalled":
+            ins = move(e, cut(T.dn, a[0] * 4 + a[1], 64), ps[:, 0:64])
+        elif kind == "table":
+            ins = g.sync.dma_start(T["tb%d" % a[0]][0:128:16, P + G * a[1]:P + G * (a[1] + 1)], cut(T.dn, a[0] * 4 + a[1], 64))
+        elif kind[0] in "qp":
+            r, l = a[:2]
+            z, tb = r * 4 + l, T["tb%d" % r]
+            first = r == 0 and l < 3
+            if kind == "qgather":
+                x = T.tp16[:, 16 * q:16 * q + 16] if r == 0 else mine(T["xl%d" % (r - 1)], l)
+                ins = move(e, cut(T.gq, z, Q), T.t4[:, 0:P + G * (l + 1)].indirect(x))
+            elif kind == "qpe":
+                for j in range(4):
+                    ins = g.tensor.matmul(ps[:, 0:64], T.zq[:, 3 - j:131 - j], T.gq[:, z * Q + j:z * Q + Q:4], j == 0, j == 3)
+            elif kind == "qconv": ins = move(e, cut(T.xw, z, 64), ps[:, 0:64])
+            elif kind == "pgather":
+                k, win = a[2], tb[:, 0:P + G * (l + 1)]
+                if first: ins = move(e, cut(T.gp, 4 * z + k + 1, Q), win.indirect(cut(T.xs, 4 * k - 4 + l, 16) if k else mine(T.cd16, l)))
+                else: ins = move(e, cut(T.gp, 2 * z + k, H), win.indirect(cut(T.xw, 2 * z + k, 32)))
+            elif kind == "prows":
+                ins = g.tensor.matmul(ps[:, 0:Q], T.eye[:], own(T.t4, l) if first else cut(T.gq, z, Q), True, False)
+            elif kind == "pflags":
+                for k in range(4):
+                    fk = T.fm[:, 16 - k:144 - k]
+                    if first: ins = g.tensor.matmul(ps[:, 0:Q], fk, cut(T.gp, 4 * z + k, Q) if k else own(tb, l), False, k == 3)
+                    else:
+                        for j in range(4):
+                            ins = g.tensor.matmul(ps[:, j:Q:4], fk, T.gp[:, z * G + 4 * k + j:z * G + G:16], False, k + j == 6)
+            elif kind == "prelu":
+                out = own(T.tb3, l) if (r == RO - 1 and l < 3) else cut(T.gr, z, Q)
+                if e == "V": ins = ts(out, ps[:, 0:Q], 0.0, None, A.max)
+                else: ins = g.scalar.activation(out, ps[:, 0:Q], F.Relu)
+            elif kind == "ppe": ins = compact(ps[:, 0:16], 4, T.gr, z * Q, 16)
+            else: ins = move(e, mine(T["xl%d" % r], l) if r < RO - 1 else T.yts[:, 16 * q:16 * q + 16], ps[:, 0:16])
         elif kind == "hop3":
             r, l = a
-            c0 = 64 * l + 16 * q
-            if r < RO - 1: part = T["xl%d" % r][:, c0:c0 + 16]
-            elif l < 3: part = T.r3[:, own(l):own(l) + Q]
-            else: part = T.yts[:, 16 * q:16 * q + 16]
-            spread(name, lambda p: (part, part))
+            spread(name, mine(T["xl%d" % r], l) if r < RO - 1 else own(T.tb3, l) if l < 3 else T.yts[:, 16 * q:16 * q + 16])
         elif kind == "u":
             r, l, h = a
-            at, c0 = P + G * l + 512 * h, 64 * l + 32 * h
-            ins = move(e, T["u%d" % r][:, at:at + 512], T["v%d" % r][:, 0:at + 512].indirect(T["xl%d" % (r - 1)][:, c0:c0 + 32]))
+            at, c0 = P + G * l + H * h, 64 * l + 32 * h
+            ins = move(e, T["u%d" % r][:, at:at + H], T["v%d" % r][:, 0:at + H].indirect(T["xl%d" % (r - 1)][:, c0:c0 + 32]))
         elif kind == "np":
             r, h = a
             x = T.tp16[:, 32 * h:32 * h + 32] if r == 0 else T.xl0[:, 192 + 32 * h:224 + 32 * h]
-            ins = move(e, T["v%d" % (r + 1)][:, 512 * h:512 * h + 512], T["v%d" % r][:, 0:W].indirect(x))
+            ins = move(e, T["v%d" % (r + 1)][:, H * h:H * h + H], T["v%d" % r][:, 0:W].indirect(x))
         elif kind == "storet":
             ins = g.sync.dma_start(T.yt[:], T.yts[:])
         elif kind == "y0":
             ins = g.vector.tensor_copy(T["y%ss" % a[0][1]][:, 0:64], T[a[0] + "32"][:, 0:64])
         elif kind == "fgather":
             t, l, h = a
-            at, c0 = ((l - 1) * 2 + (t == "fb")) * G + 512 * h, 64 * l + 32 * h
-            ins = move(e, T.gf[:, at:at + 512], T.r3[:, 0:P + G * l].indirect(T[t + "16"][:, c0:c0 + 32]))
+            at, c0 = ((l - 1) * 2 + (t == "fb")) * G + H * h, 64 * l + 32 * h
+            ins = move(e, T.gf[:, at:at + H], T.tb3[:, 0:P + G * l].indirect(T[t + "16"][:, c0:c0 + 32]))
         elif kind == "fpe":
             t, l = a
-            ins = compact(ps, T.gf, ((l - 1) * 2 + (t == "fb")) * G, 64)
+            ins = compact(ps[:, 0:64], 4, T.gf, ((l - 1) * 2 + (t == "fb")) * G, 64)
         elif kind == "fcopy":
             t, l = a
             ins = move(e, T["y%ss" % t[1]][:, 64 * l:64 * l + 64], ps[:, 0:64])

@@ -7,20 +7,25 @@ W = P + L * G
 Q = G // N
 H = G // 2
 BIG = 128
+EARLY = 2
 
 SCRATCH = {}
 for _names, _cols, _dt in (
         ("v0 v1 v2 tb0 tb1 tb2 t1 t4", W, "bfloat16"), ("u1 u2 tb3", 4096, "bfloat16"), ("df gp", 12 * G, "bfloat16"),
-        ("gs gq gr", 12 * Q, "bfloat16"), ("gf", 6 * G, "bfloat16"), ("cnt", 12 * 4 * 64, "bfloat16"), ("dn", 12 * 64, "bfloat16"),
-        ("nd", 640, "bfloat16"), ("jt", 512, "bfloat16"), ("bk", G, "bfloat16"), ("one neg zs zw1 zw4 zq dm", 144, "bfloat16"),
-        ("fm", 160, "bfloat16"), ("eye jb", 128, "bfloat16"), ("b16", 16, "bfloat16"), ("fa32 fb32 cd32", 256, "int32"),
-        ("tp32 nn n2 jd", 64, "int32"), ("ja", 128, "int32"), ("ip ib", 8, "int32"), ("fa16 fb16 cd16 xl0 xl1", 256, "uint16"),
-        ("tp16", 64, "uint16"), ("xs", 128, "uint16"), ("xw", 12 * 64, "uint16"), ("yas ybs", 256, "float32"),
-        ("yts xx", 64, "float32"), ("cc kc gm wt", 16, "float32")):
+        ("gq gr", 12 * Q, "bfloat16"), ("gs", 20 * Q, "bfloat16"), ("gf", 6 * G, "bfloat16"), ("cnt", 12 * 4 * 64, "bfloat16"), ("dn", 12 * 64, "bfloat16"),
+        ("nd", 640, "bfloat16"), ("jt", 512, "bfloat16"), ("bk", 256, "bfloat16"), ("one neg zs zw1 zw4 zq dm", 144, "bfloat16"),
+        ("fm", 160, "bfloat16"), ("eye", 128, "bfloat16"), ("b16", 16, "bfloat16"), ("fa32 fb32 cd32", 256, "int32"),
+        ("tp32 cq nn n2 jd", 64, "int32"), ("ja", 128, "int32"), ("ip ib", 8, "int32"), ("fa16 fb16 cd16 xl0 xl1", 256, "uint16"),
+        ("tp16", 64, "uint16"), ("xs", 20 * 16, "uint16"), ("xw", 12 * 64, "uint16"), ("yas ybs", 256, "float32"),
+        ("yts xx xk wt", 64, "float32"), ("gm", 32, "float32"), ("cc kc", 16, "float32")):
     for _n in _names.split():
         SCRATCH[_n] = ("sbuf", [128, _cols], _dt)
 for _b in range(8):
     SCRATCH["ps%d" % _b] = ("psum", [128, 512], "float32")
+
+
+def parts(r, l):
+    return [(0, H), (H, Q), (H + Q, Q)] if (r == RO - 1 and l >= 2) else [(0, H), (H, H)]
 
 
 def build_ops():
@@ -39,55 +44,55 @@ def build_ops():
 
     op("lx", "load", "Y", "dma", 2048, [], ("x", 0, P))
     for t in ("fb", "fa"):
-        op("l%s0" % t, "load", "YS", "dma", 256, [], (t, 0, 64))
-        op("l%s1" % t, "load", "YS", "dma", 768, [], (t, 64, 256))
+        op("l%s0" % t, "load", "S", "dma", 256, [], (t, 0, 64))
+        op("l%s1" % t, "load", "Y", "dma", 768, [], (t, 64, 256))
         op("c%s0" % t, "conv", "V", "c1", 64, ["l%s0" % t], (t, 0, 64))
         op("c%s1" % t, "conv", "V", "c1", 192, ["l%s1" % t], (t, 64, 256))
-    op("lcd", "load", "YS", "dma", 1024, [], ("cd", 0, 256))
+    op("lcq", "loadq", "Y", "dma", 256, [])
+    op("lcd", "load", "S", "dma", 1024, [], ("cd", 0, 256))
     op("ccd0", "conv", "V", "c1", 64, ["lcd"], ("cd", 0, 64))
     op("ccd1", "conv", "V", "c1", 192, ["lcd"], ("cd", 64, 256))
     op("ltp", "load", "Y", "dma", 256, [], ("tp", 0, 64))
     op("ctp", "conv", "V", "c1", 64, ["ltp"], ("tp", 0, 64))
-    op("lfill", "fill", "Y", "dma", 2048, [])
     lst = lambda t, l: "c%s%d" % (t, min(l, 1))
     for t, n, d in (("ip", 1, []), ("xx", 64, []), ("nn", 64, []), ("one", 144, []), ("zs0", 144, ["one"]), ("zs", 144, ["zs0"]),
                     ("eye", 128, ["one"]), ("dm", 136, ["one"]), ("neg", 144, []), ("fm0", 144, ["neg"]), ("fm", 144, ["fm0"]),
-                    ("zq", 144, [])):
+                    ("zq0", 144, []), ("xk", 64, []), ("gm0", 32, ["one"]), ("gm", 32, ["gm0"])):
         op(t, "pool", "G", "pool", n, d, (t,))
-    for t, n, d in (("ib", 1, ["ip"]), ("i8", 1, ["ip"]), ("bf", 2, ["ib", "i8"]), ("al", 1, ["ib"]), ("be", 1, ["ib"]),
-                    ("ga", 1, ["ib", "al"]), ("kc", 9, ["al", "xx"]), ("nd0", 64, ["be", "ga", "xx"]), ("b16", 16, ["bf", "xx"]),
-                    ("n2", 64, ["bf", "nn"]), ("ws", 1, ["al"]), ("w0", 1, ["i8"]), ("wk", 5, ["bf", "xx"]),
-                    ("wt", 5, ["ws", "w0", "wk"]), ("jd", 64, ["n2", "lcd"]), ("jh", 64, ["jd"]), ("jl", 64, ["jd"]),
-                    ("jb", 128, ["jh", "jl"])):
+    for t, n, d in (("ib", 1, ["ip"]), ("i8", 1, ["ip"]), ("od", 1, ["ip"]), ("bf", 3, ["ib", "i8", "od"]), ("ev", 1, ["od"]),
+                    ("al", 1, ["ib"]), ("be", 1, ["ib"]), ("ga", 1, ["ib", "al"]), ("kc", 9, ["al", "xx"]),
+                    ("nd0", 64, ["be", "ga", "xx"]), ("b16", 16, ["bf", "xx"]), ("n2", 64, ["bf", "nn"]), ("ws", 1, ["al"]),
+                    ("w0", 1, ["i8"]), ("wk", 40, ["bf", "xk"]), ("wt", 40, ["ws", "w0", "wk"]), ("zq", 32, ["zq0", "gm", "wt"]),
+                    ("jd", 64, ["n2", "lcq"]), ("jh", 64, ["jd"]), ("jl", 64, ["jd"]), ("bk0", 128, ["jh", "jl", "ev"]),
+                    ("bk1", 128, ["jh", "jl", "bf"])):
         op(t, "tiny", "V", "c1", n, d, (t,))
-    op("gm", "tiny", "VS", "c1", 8, ["zs"], ("gm",))
     for k in (1, 4):
         op("zw%d" % k, "zw", "VS", "ch", 144, ["zs", "wt"], (k,))
-    for k in range(4):
-        op("zq%d" % k, "zq", "VS", "c1", 8, ["zq", "gm", "wt"], (k,))
     for k, (at, n) in enumerate(((64, 64), (128, 128), (256, 256), (512, 128))):
         op("nd%d" % (k + 1), "dbl", "VS", "ch", n, ["nd%d" % min(k, 2), "kc"], (at, n))
     op("zero", "zero", "V", "ch", P, [])
     for l in range(L):
-        op("fz%d" % l, "fillz", "Y", "dma", 2048, ["zero"], (l,))
+        op("fz%d" % l, "fillz", "SY", "cp", G, ["zero"], (l,))
     op("tn", "names", "Y", "dma", 1280, ["nd3", "nd4"] + ["fz%d" % l for l in range(L)])
-    for b in range(8):
-        op("bk%d" % b, "block", "VS", "ch", 128, ["jb", "gm"], (b,))
-    job(["turn", "jt"], ["turn", "turned"], [8 * 64, 128], [["bk%d" % b for b in range(8)] + ["b16"], []], "VS", ())
+    job(["turn", "jt"], ["turn", "turned"], [32 * 32, 128], [["bk0", "bk1", "b16"], []], "VS", ())
     op("h0_", "hop0", "G", "hop", 256, ["jt"])
     for l in range(L):
         op("tj%d" % l, "jump", "Y", "dma", 256, ["jt", "h0_", "fz%d" % l], (l,))
-    op("it4", "ident", "Y", "dma", 2048, ["tn"], ("t4",))
-    op("it3", "ident", "Y", "dma", 2048, ["tn"], ("tb3",))
-    tab = ["tn"] + ["tj%d" % l for l in range(L)]
-    got = [["sg0%d" % l for l in range(L)], ["sg10", "sg11"], ["sg20", "sg21"]]
-    for s in range(3):
-        for k, n in enumerate(got[s]):
-            op(n, "sgather", "VS", "g", G // len(got[s]), tab[:k + 2] + [lst("cd", k)] if s == 0 else tab + ["sc%d" % (s - 1)], (s, k))
-        if s < 2: job(["sp%d" % s, "sc%d" % s], ["spe", "sconv"], [16 * 64, 64], [got[s] + ["zw1"], []], "V", (s,))
-    for l in range(L):
-        job(["st%d" % l, "sq%d" % l], ["stack", "stacked"], [4 * Q, Q], [["sc1", "sg2%d" % (l // 2), "eye", "dm"], []], "VS", (l,))
-        op("hs%d" % l, "hops", "G", "hop", 512, ["sq%d" % l], (l,))
+    op("it4", "ident", "YS", "cp", G, ["tn"], ("t4",))
+    op("it3", "ident", "YS", "cp", G, ["tn"], ("tb3",))
+
+    def follow(z, steps, tab, x):
+        for s in steps:
+            op("sg%d%d" % (z, s), "sgather", "VS", "g", Q, tab + [x], (z, s))
+            if s < 3:
+                x = "sc%d%d" % (z, s)
+                job(["sp%d%d" % (z, s), x], ["spe", "sconv"], [16 * 64, 16], [["sg%d%d" % (z, s), "zw1"], []], "V", (z, s))
+        if z < L:
+            job(["st%d" % z, "sq%d" % z], ["stack", "stacked"], [4 * Q, Q], [["sg%d3" % z, "eye", "dm"], []], "VS", (z,))
+            op("hs%d" % z, "hops", "G", "hop", 512, ["sq%d" % z], (z,))
+
+    for l in range(EARLY):
+        follow(l, (1, 2, 3), ["tn"] + ["tj%d" % k for k in range(l + 1)], lst("cd", l))
 
     for r in range(RO):
         inp = ["lx"] if r == 0 else ["np%d_0" % (r - 1), "np%d_1" % (r - 1)]
@@ -96,34 +101,42 @@ def build_ops():
         src = list(inp)
         for l in range(L):
             rl, a = "%d%d" % (r, l), (r, l)
-            low = inp + ["A%d%d%d" % (r, k, h) for k in range(l) for h in range(2)]
-            both = ["A%s0" % rl, "A%s1" % rl]
-            for h in range(2):
-                op("B%s%d" % (rl, h), "B", "VS", "g", H, src + [lst("fb", l)], (r, l, h))
-                op("A%s%d" % (rl, h), "A", "V", "g", H, src + [lst("fa", l), "B%s%d" % (rl, h)], (r, l, h))
-                op("cp%s%d" % (rl, h), "shadow", "YGVS", "cp", H, ["A%s%d" % (rl, h)], (r, l, h))
-                op("vo%s%d" % (rl, h), "vote", "V", "g", H, low + both[:h + 1] + ["cp%s%d" % (rl, h), lst("cd", l)], (r, l, h))
+            low = inp + ["A%d%d%d" % (r, k, h) for k in range(l) for h in range(len(parts(r, k)))]
+            both = ["A%s%d" % (rl, h) for h in range(len(parts(r, l)))]
+            for h, (c, n) in enumerate(parts(r, l)):
+                op("B%s%d" % (rl, h), "B", "VS", "g", n, src + [lst("fb", l)], (r, l, c, n))
+                op("A%s%d" % (rl, h), "A", "V", "g", n, src + [lst("fa", l), "B%s%d" % (rl, h)], (r, l, c, n))
+                op("cp%s%d" % (rl, h), "shadow", "YGVS", "cp", n, ["A%s%d" % (rl, h)], (r, l, c, n))
+                op("vo%s%d" % (rl, h), "vote", "V", "g", n, low + both[:h + 1] + ["cp%s%d" % (rl, h), lst("cd", l)], (r, l, c, n))
             if r == RO - 1:
                 if l == 0:
                     op("sv0", "storev", "Y", "dma", 2048, inp, (0,))
                 op("sv%d" % (l + 1), "storev", "Y", "dma", 2048, both, (l + 1,))
-            job(["su" + rl, "sw" + rl, "cn" + rl], ["sum0", "sum1", "count"], [8 * 64, 8 * 64, 64],
-                [["vo%s0" % rl, "zs"], ["vo%s1" % rl], []], "VS", a)
+            job(["su%s%d" % (rl, h) for h in range(len(both))] + ["cn" + rl], ["sum%d" % h for h in range(len(both))] + ["count"],
+                [n for c, n in parts(r, l)] + [64], [["vo%s%d" % (rl, h), "zs"] for h in range(len(both))] + [[]], "VS", a)
             op("h1_" + rl, "hop1", "G", "hop", 128, ["cn" + rl], a)
             job(["ex" + rl, "mi" + rl], ["total", "totalled"], [4 * 64, 64], [["cn" + rl, "h1_" + rl, "eye"], []], "VS", a)
-            op("tw" + rl, "table", "Y", "dma", 128, ["mi" + rl], a)
-            tab = ["lfill" if r == 0 else "sw%d0" % (r - 1)] + ["tw%d%d" % (r, k) for k in range(l + 1)]
-            if r == 0 and l < 3:
-                rows, look = "sq%d" % l, [(Q, lst("cd", l)), (Q, "sc0"), (Q, "sc1")]
+            op("tw" + rl, "table", "Y", "dma", 128, ["mi" + rl] + (["tn", "tj%d" % l] + ["sg%d3" % k for k in range(l, EARLY)] + ["st%d" % l] * (l < EARLY)) * (r == 0), a)
+            tab = ["tw%d%d" % (r, k) for k in range(l + 1)]
+            if r == 0 and l < EARLY:
+                for s in (1, 2, 3):
+                    op("pg%s%d" % (rl, s), "again", "VS", "g", Q, tab + ["sg%d%d" % (l, s)], (l, s))
+                job(["pa" + rl, "pb" + rl, "pr" + rl], ["prows", "pagain", "prelu"], [Q, 4 * Q, Q],
+                    [["sq%d" % l], ["pg%s%d" % (rl, s) for s in (1, 2, 3)] + ["fm"], []], "VS", a)
+            elif r == 0:
+                follow(l, (1, 2, 3), tab, lst("cd", l))
+                z = l + (l == 3)
+                if l == 3: follow(z, (0, 1, 2, 3), tab, "ctp")
+                job(["pa" + rl, "pb" + rl, "pc" + rl, "pr" + rl], ["pstep0", "pstep1", "pstep2", "prelu"], [4 * Q, 2 * Q, 2 * Q, Q],
+                    [["sg%d1" % z, "eye", "dm", "fm"], ["sg%d2" % z], ["sg%d3" % z], []], "VS", a)
             else:
-                x0 = "ctp" if r == 0 else "pl%d%d" % (r - 1, l)
-                rows, look = "qg" + rl, [(H, "qc" + rl), (H, "qc" + rl)]
-                op(rows, "qgather", "VS", "g", Q, ["it4", x0] + [t + str(k) for k in range(l + 1) for t in ("sq", "hs")], a)
-                job(["qa" + rl, "qc" + rl], ["qpe", "qconv"], [4 * 64, 64], [[rows] + ["zq%d" % k for k in range(4)], []], "V", a)
-            for k, (n, x) in enumerate(look):
-                op("pg%s%d" % (rl, k), "pgather", "VS", "g", n, tab + [x], (r, l, k))
-            job(["pa" + rl, "pb" + rl, "pr" + rl], ["prows", "pflags", "prelu"], [Q, 4 * Q, Q],
-                [[rows, "eye"], ["pg%s%d" % (rl, k) for k in range(len(look))] + ["fm"], ["it3"] * (r == RO - 1 and l < 3)], "VS", a)
+                op("qg" + rl, "qgather", "VS", "g", Q,
+                   ["it4", "pl%d%d" % (r - 1, l)] + [t + str(k) for k in range(l + 1) for t in ("sq", "hs")], a)
+                job(["qa" + rl, "qc" + rl], ["qpe", "qconv"], [4 * 64, 64], [["qg" + rl, "zq"], []], "V", a)
+                for k in range(2):
+                    op("pg%s%d" % (rl, k), "pgather", "VS", "g", H, tab + ["cn%d0" % (r - 1), "qc" + rl], (r, l, k))
+                job(["pa" + rl, "pb" + rl, "pr" + rl], ["prows", "pflags", "prelu"], [Q, 4 * Q, Q],
+                    [["qg" + rl, "eye"], ["pg%s0" % rl, "pg%s1" % rl, "fm"], ["it3"] * (r == RO - 1 and l < 3)], "VS", a)
             x = "pr" + rl
             if r < RO - 1 or l == 3:
                 x = "pl" + rl
@@ -135,10 +148,10 @@ def build_ops():
             else:
                 for h in range(2):
                     op("u%s%d" % (rl, h), "u", "VS", "g", H,
-                       low + both[:h + 1] + ["h3_%d%d" % (r - 1, l), "pl%d%d" % (r - 1, l)], (r, l, h))
+                       low + (both if h else both[:1]) + ["h3_%d%d" % (r - 1, l), "pl%d%d" % (r - 1, l)], (r, l, h))
                 src = ["iu%d" % r] + ["u%d%d%d" % (r, k, h) for k in range(l + 1) for h in range(2)]
         if r < RO - 1:
-            allv = inp + ["A%d%d%d" % (r, k, h) for k in range(L) for h in range(2)]
+            allv = low + both
             for h in range(2):
                 op("np%d_%d" % (r, h), "np", "VS", "g", H, allv + (["ctp"] if r == 0 else ["h3_03", "pl03"]), (r, h))
     op("syt", "storet", "Y", "dma", 256, ["h3_23", "pl23"])
@@ -159,17 +172,19 @@ OPS = build_ops()
 SEMAPHORES = ["cV", "cS", "cP", "cG", "sent"] + ["s_" + n for n, o in OPS.items() if o["cost"] in ("dma", "hop", "cp")]
 
 GUESSES = [dict(zip("cycle gather pe call sem issue start rissue rstart row byte first".split(), v)) for v in (
-    (0.00104, 0.0012, 0.00056, 0.06, 0.1, 0.2, 1.0, 0.6, 1.0, 0.02, 0.00004, 2.0),
-    (0.0012, 0.0012, 0.00066, 0.07, 0.1, 0.3, 0.6, 0.9, 1.3, 0.015, 0.00004, 2.0),
-    (0.0009, 0.0015, 0.0005, 0.04, 0.1, 0.1, 1.5, 0.6, 1.0, 0.04, 0.00006, 1.0))]
-LEAN, SWEEPS, STEPS = 0.8, 6, 50000
+    (0.00096, 0.0014, 0.00055, 0.0, 0.09, 0.25, 0.85, 0.2, 1.4, 0.024, 0.000035, 0.5),
+    (0.001, 0.0012, 0.0005, 0.02, 0.07, 0.4, 1.0, 0.9, 1.5, 0.035, 0.00003, 2.5),
+    (0.0009, 0.0011, 0.0005, 0.02, 0.13, 0.3, 1.3, 0.4, 0.7, 0.012, 0.00004, 1.2))]
+QUEUES = "VSPGY"
+OPENING = "lx lfb0 lcq lfa0 lcd lfb1 lfa1".split()
+LEAN, SWEEPS, STEPS, HEAT = 0.8, 6, 320000, 0.004
 
 
 def needs(o, e, m):
     c, n = o["cost"], o["n"]
     if c == "dma" or (c == "cp" and e == "Y"): return m["issue"], m["start"], 8 * (m["row"] + n * m["byte"] * (2 if c == "cp" else 1))
     if c == "hop": return m["rissue"], m["rstart"], 32 * (m["row"] + n * m["byte"])
-    if c == "g": return m["call"] + n * m["gather"], 0, 0
+    if c == "g": return 0.055 + n * m["gather"], 0, 0
     if c == "pe": return n * m["pe"], 0, 0
     if e == "G": return 0.16 + 2 * n * m["cycle"], 0, 0
     return m["call"] + max(64, n // 2 if (c in ("ch", "cp") and e == "V") else n) * m["cycle"], 0, 0
@@ -216,30 +231,63 @@ def with_banks(order, eng):
     return order, eng, bank, extra
 
 
-def replay(plan, deps, costs, m):
-    free, last, done, why = dict.fromkeys("VSPGY", 0.0), dict.fromkeys("VSPGYD"), {}, {}
-    dma, first, sem, extra, eng = 0.0, m["first"], m["sem"], plan[3], plan[1]
-    for n in plan[0]:
+def behind(order, eng, users, cost, m, run, old, same):
+    rest, issue, nxt, dma, sem = list(old[3]), list(old[5]), [0.0] * 5, 0.0, m["sem"]
+    for n in order[same + 60:same:-1]:
+        nxt[eng[n]] = issue[n] - sem
+        if cost[n][eng[n]][2]: dma = rest[n] + cost[n][eng[n]][2]
+    for n in order[same::-1]:
+        e = eng[n]
+        hold, off, d = cost[n][e]
+        t = dma if d else 0.0
+        for x in users[n]:
+            if issue[x] > t: t = issue[x]
+        rest[n] = t
+        if d: dma = t = t + d
+        t += off if d else hold
+        if hold + nxt[e] > t: t = hold + nxt[e]
+        nxt[e], issue[n] = t, t + sem
+    n, pairs, why = run[0].index(max(run[0])), [], run[1]
+    while n is not None:
+        if why[n][1] and why[n][0] is not None: pairs.append((why[n][0], n))
+        n = why[n][0]
+    return run + (rest, pairs, issue)
+
+
+def replay(order, eng, extra, deps, cost, m, old, at, same, bound, used):
+    at -= at % 16
+    done, why, marks = list(old[0]), list(old[1]), old[2][:at // 16 + 1]
+    free, last, dma, first = marks[-1]
+    free, last, sem, was, rest, reach = list(free), list(last), m["sem"], old[0], old[3], max(same, used[0])
+    for i in range(at, len(order)):
+        n = order[i]
+        if i % 16 == 0 and i > at:
+            marks.append((tuple(free), tuple(last), dma, first))
+            if i > reach and marks[-1] == old[2][i // 16]: return done, why, marks + old[2][i // 16 + 1:]
         e = eng[n]
         t, w, queued = free[e], last[e], True
         for d in deps[n] + [extra[n]] if n in extra else deps[n]:
             if done[d] + sem > t: t, w, queued = done[d] + sem, d, False
-        hold, off, d = costs[n, e]
-        if d and e == "G": t, first = t + first, 0.0
-        free[e] = done[n] = t + hold
+        hold, off, d = cost[n][e]
         if d:
-            if dma > t + off: w, queued = last["D"], True
-            dma = done[n] = max(dma, t + off) + d
-            last["D"] = n
-        last[e], why[n] = n, (w, queued)
-    end = max(done, key=done.get)
-    return done[end], end, why
+            if e == 3: t, first = t + first, 0.0
+            if dma > t + off: w, queued = last[5], True
+            else: dma = t + off
+            dma = done[n] = dma + d
+            last[5] = n
+        else: done[n] = t + hold
+        if done[n] != was[n]:
+            if i > same and done[n] + rest[n] > bound: return None
+            if used[n] > reach: reach = used[n]
+        free[e], last[e], why[n] = t + hold, n, (w, queued)
+    return done, why, marks
 
 
 def make_plan():
     before = {n: o["deps"] for n, o in OPS.items()}
     after = {n: [x for x in OPS if n in before[x]] for n in OPS}
-    index = {n: i for i, n in enumerate(OPS)}
+    names = list(OPS)
+    index = {n: i for i, n in enumerate(names)}
     start, end, eng = sweep(index, before, False)
     for k in range(SWEEPS):
         start, end, eng = sweep({n: -end[n] for n in OPS}, after, True)
@@ -247,52 +295,79 @@ def make_plan():
     below = {}
     for n in OPS:
         below[n] = set(before[n]).union(*[below[d] for d in before[n]])
-    deps = {n: [d for d in dict.fromkeys(before[n]) if not any(d in below[x] for x in before[n])] for n in OPS}
-    costs = [{(n, e): needs(o, e, m) for n, o in OPS.items() for e in o["eng"]} for m in GUESSES]
+    deps = [[index[d] for d in dict.fromkeys(before[n]) if not any(d in below[x] for x in before[n])] for n in names]
+    users = [[i for i, d in enumerate(deps) if k in d] for k in range(len(names))]
+    may = [[QUEUES.index(e) for e in OPS[n]["eng"]] for n in names]
+    costs = [[[needs(OPS[n], e, m) if e in OPS[n]["eng"] else None for e in QUEUES] for n in names] for m in GUESSES]
+    role = [OPS[n]["bank"].index(n) + 1 if n in (OPS[n]["bank"] or ()) else 0 for n in names]
     state = [12345]
 
     def draw(k):
         state[0] = (state[0] * 1103515245 + 12345) % 2 ** 31
         return (state[0] >> 8) % k
 
-    def weigh(plan):
-        runs = [replay(plan, deps, c, m) for c, m in zip(costs, GUESSES)]
-        return sum(x[0] for x in runs) / len(runs), runs
+    def waits(order):
+        free, extra = [None] * 8, {}
+        for n in order:
+            if role[n] == 2: free.append(n)
+            elif role[n]:
+                if not free: return None
+                if free[0] is not None: extra[n] = free[0]
+                del free[0]
+        return extra
 
-    plan = with_banks(sorted(OPS, key=lambda n: (start[n], index[n])), eng)
-    now, runs = weigh(plan)
-    best = (now, plan)
+    def last_use(order, extra):
+        used = [0] * len(order)
+        for i, n in enumerate(order):
+            for d in deps[n]: used[d] = i
+            if n in extra: used[extra[n]] = i
+        return used
+
+    order = [index[n] for n in OPENING + sorted(set(OPS) - set(OPENING), key=lambda n: (start[n], index[n]))]
+    eng = [QUEUES.index(eng[n]) for n in names]
+    zeros = [0.0] * len(names)
+    empty = lambda m: (zeros, [None] * len(names), [([0.0] * 5, [None] * 6, 0.0, m["first"])], zeros, [], zeros)
+    runs = [behind(order, eng, users, c, m, replay(order, eng, waits(order), deps, c, m, empty(m), 0, len(order), 0, zeros), empty(m), len(order))
+            for c, m in zip(costs, GUESSES)]
+    scale = [1.0 / max(x[0]) for x in runs]
+    now = [1.0] * len(runs)
+    best, held = (sum(now), order, eng), waits(order)
+    used, never = last_use(order, held), [len(order)] * len(order)
     for step in range(STEPS):
-        total, n, why = runs[draw(len(runs))]
-        pairs = []
-        while n:
-            if why[n][0] and why[n][1]: pairs.append((why[n][0], n))
-            n = why[n][0]
+        pairs = runs[draw(len(runs))][4]
         a, b = pairs[draw(len(pairs))]
-        order, eng, how = plan[0], plan[1], draw(10)
+        order2, eng2, how = order, eng, draw(10)
         if how < 3:
             n = (a, b, order[draw(len(order))])[how]
-            eng = dict(eng)
-            eng[n] = OPS[n]["eng"][draw(len(OPS[n]["eng"]))]
-            if eng[n] == plan[1][n]: continue
+            eng2 = list(eng)
+            eng2[n] = may[n][draw(len(may[n]))]
+            if eng2[n] == eng[n]: continue
+            i = j = order.index(n)
         else:
-            far = (0, 0, 4, 10, 25)[draw(5)]
+            far = (0, 0, 4, 10, 25, 60)[draw(6)]
             i, j = order.index(a), order.index(b)
-            if how < 7: i, keep, links, part = max(0, i - far), {b}, deps, order[max(0, i - far):j + 1][::-1]
-            else: j, keep, links, part = j + far, {a}, after, order[i:j + far + 1]
+            if how < 7: i, keep, links, part = i - far, {b}, deps, order[max(0, i - far):j + 1][::-1]
+            else: j, keep, links, part = j + far, {a}, users, order[i:j + far + 1]
             for n in part:
                 if n in keep: keep.update(links[n])
-            if a in keep and b in keep: continue
-            part = order[i:j + 1]
-            order = order[:i] + sorted(part, key=lambda n: (n in keep) != (how < 7)) + order[j + 1:]
-        new = with_banks(order, eng)
-        if new is None: continue
-        total, tried = weigh(new)
-        heat = 0.06 * (0.2 ** (step / STEPS))
-        if total <= now or draw(10000) < 10000 * math.exp((now - total) / heat):
-            now, runs, plan = total, tried, new
-            if now < best[0]: best = (now, plan)
-    return best[1]
+            if i < len(OPENING) or (a in keep and b in keep): continue
+            order2 = order[:i] + sorted(order[i:j + 1], key=lambda n: (n in keep) != (how < 7)) + order[j + 1:]
+        extra = waits(order2) if how > 2 and any(role[n] for n in keep) else held
+        if extra is None: continue
+        limit = sum(now) - HEAT * 0.1 ** (step / STEPS) * math.log((draw(10000) + 1) / 10001.0)
+        tried, new = [], []
+        for k in range(len(runs)):
+            room = limit - sum(new) - sum(now[k + 1:]) + 0.004 * (len(runs) - 1 - k)
+            tried.append(replay(order2, eng2, extra, deps, costs[k], GUESSES[k], runs[k], i, j, room / scale[k],
+                                used if extra == held else never))
+            if tried[k] is None: break
+            new.append(max(tried[k][0]) * scale[k])
+        if len(new) == len(runs) and sum(new) <= limit:
+            if order2 is not order: used = last_use(order2, extra)
+            now, order, eng, held = new, order2, eng2, extra
+            runs = [behind(order, eng, users, c, m, x, y, j) for c, m, x, y in zip(costs, GUESSES, tried, runs)]
+            if sum(now) < best[0]: best = (sum(now), order, eng)
+    return with_banks([names[n] for n in best[1]], {n: QUEUES[best[2][index[n]]] for n in names})
 
 
 PLAN = make_plan()
@@ -340,7 +415,6 @@ def rank_program(g, core, T, topo):
     def move(e, out, src):
         if e == "V": return g.vector.tensor_copy(out, src)
         if e == "S": return g.scalar.activation(out, src, F.Copy)
-        if e == "G": return g.affine_select(out, src, [[0, H]], A.is_ge, 0.0, 0, 0)
         return g.sync.dma_start(out, src)
 
     def scaled(e, out, src, m):
@@ -365,9 +439,11 @@ def rank_program(g, core, T, topo):
 
     col = lambda t, j: t[:, j:j + 1]
     cut = lambda t, k, n, m=1: t[:, k * n:(k + m) * n]
-    cc = {k: col(T.cc, j) for j, k in enumerate(("bf", "mf", "al", "be", "ga", "ws", "w0"))}
+    cc = {k: col(T.cc, j) for j, k in enumerate(("bf", "mf", "od", "ev", "al", "be", "ga", "ws", "w0"))}
     own = lambda t, l: t[:, P + G * l + Q * q:P + G * l + Q * q + Q]
     mine = lambda t, l: t[:, 64 * l + 16 * q:64 * l + 16 * q + 16]
+    step = lambda z, s: own(T.t1, z) if (s == 0 and z < L) else cut(T.gs, 4 * z + s, Q)
+    shift = lambda s: T.dm[:, 3 - s:131 - s] if s else T.eye[:]
     cnt = lambda r, l, p: cut(T.cnt, (r * 4 + l) * 4 + p, 64)
     df = lambda r, l, a, b: T["tb%d" % (r + 1)][:, a:b] if (l == 0 and r < RO - 1) else T.df[:, (r * 4 + l) * G + a:(r * 4 + l) * G + b]
 
@@ -380,8 +456,8 @@ def rank_program(g, core, T, topo):
         ins = None
         if kind == "load":
             ins = queue[e].dma_start((T.v0 if a[0] == "x" else T[a[0] + "32"])[:, a[1]:a[2]], T[a[0]][:, a[1]:a[2]])
-        elif kind == "fill":
-            ins = g.sync.dma_start(T.tb0[:, 0:P], T.x[:])
+        elif kind == "loadq":
+            ins = queue[e].dma_start(T.cq[:], cut(T.cd, q, 64))
         elif kind == "conv":
             ins = g.vector.tensor_copy(T[a[0] + "16"][:, a[1]:a[2]], T[a[0] + "32"][:, a[1]:a[2]])
         elif kind == "pool":
@@ -389,18 +465,23 @@ def rank_program(g, core, T, topo):
             if t == "ip": ins = g.iota(col(T.ip, 0), [[0, 1]], 0, 1)
             elif t == "xx": ins = g.iota(T.xx[:], [[1, 64]], 0, 0, **small)
             elif t == "nn": ins = g.iota(T.nn[:], [[16, 64]], P + G * q, 0)
-            elif t in ("one", "neg", "zq"): ins = g.iota(T[t][:], [[0, 144]], {"one": 1, "neg": -BIG, "zq": 0}[t], 0, **small)
+            elif t in ("one", "neg", "zq0"): ins = g.iota(T[t[:2 + (t != "zq0")]][:], [[0, 144]], {"one": 1, "neg": -BIG, "zq0": 0}[t], 0, **small)
+            elif t == "xk": ins = g.iota(T.xk[:], [[4, 2], [0, 8], [1, 4]], 0, 0, **small)
+            elif t == "gm0": ins = g.affine_select(T.gm[:], T.one[:, 0:32], [[-16, 8], [0, 4]], A.is_ge, 0.0, 0, 1)
+            elif t == "gm": ins = g.affine_select(T.gm[:], T.gm[:], [[16, 8], [0, 4]], A.is_ge, 0.0, 15, -1)
             elif t == "zs0": ins = g.affine_select(T.zs[:], T.one[:], [[-16, 9], [1000, 16]], A.is_ge, 0.0, -15000, 1)
             elif t == "zs": ins = g.affine_select(T.zs[:], T.zs[:], [[16, 9], [0, 16]], A.is_ge, 0.0, 15, -1)
             elif t == "eye": ins = g.affine_select(T.eye[:], T.one[:, 0:128], [[-1, 128]], A.is_equal, 0.0, 0, 1)
             elif t == "dm": ins = g.affine_select(T.dm[:, 0:136], T.one[:, 0:136], [[-8, 17], [1000, 8]], A.is_equal, 0.0, -4001, 1)
-            elif t == "fm0": ins = g.affine_select(T.fm[:, 1:145], T.neg[:], [[-16, 9], [0, 16]], A.is_equal, 0.0, 16, 1)
+            elif t == "fm0": ins = g.affine_select(T.fm[:, 1:145], T.neg[:], [[-16, 9], [0, 16]], A.is_equal, 0.0, 9, 1)
             else: ins = g.affine_select(T.fm[:, 1:145], T.fm[:, 1:145], [[0, 18], [1, 2], [0, 4]], A.is_equal, 0.0, 0, 0)
         elif kind == "tiny":
             t = a[0]
             if t == "ib": ins = ts(ib, col(T.ip, 0), 15, None, A.bitwise_and)
             elif t == "i8": ins = ts(col(T.ib, 1), col(T.ip, 0), 7, None, A.bitwise_and)
-            elif t == "bf": ins = g.vector.tensor_copy(T.cc[:, 0:2], T.ib[:, 0:2])
+            elif t == "od": ins = ts(col(T.ib, 2), col(T.ip, 0), 4, 1, A.arith_shift_right, A.bitwise_and)
+            elif t == "bf": ins = g.vector.tensor_copy(T.cc[:, 0:3], T.ib[:, 0:3])
+            elif t == "ev": ins = ts(cc["ev"], col(T.ib, 2), 0.0, None, A.is_equal)
             elif t == "al": ins = ts(cc["al"], ib, 8.0, None, A.is_lt)
             elif t == "be": ins = ts(cc["be"], ib, 8.0, None, A.is_ge)
             elif t == "ga": ins = ts(cc["ga"], ib, 10.0, cc["al"], A.mult, A.mult)
@@ -410,17 +491,15 @@ def rank_program(g, core, T, topo):
             elif t == "n2": ins = ts(T.n2[:], T.nn[:], cc["bf"], None, A.add)
             elif t == "ws": ins = ts(cc["ws"], cc["al"], 63.0, 1.0, A.mult, A.add)
             elif t == "w0": ins = ts(cc["w0"], col(T.ib, 1), 0.0, 2.0, A.is_equal, A.mult)
-            elif t == "wk": ins = ts(T.wt[:, 8:13], T.xx[:, 0:5], cc["mf"], -1.0, A.is_ge, A.mult)
-            elif t == "wt": ins = ts(T.wt[:, 0:5], T.wt[:, 8:13], cc["w0"], cc["ws"], A.add, A.mult)
-            elif t == "jd": ins = g.vector.tensor_tensor(T.jd[:], T.n2[:], cut(T.cd32, q, 64), A.subtract)
+            elif t == "wk": ins = ts(T.wt[:, 0:33], T.xk[:, 0:33], cc["mf"], -1.0, A.is_ge, A.mult)
+            elif t == "wt": ins = ts(T.wt[:, 0:33], T.wt[:, 0:33], cc["w0"], cc["ws"], A.add, A.mult)
+            elif t == "zq": ins = g.vector.tensor_tensor(T.zq[:, 3:128:4], T.gm[:], T.wt[:, 0:32], A.mult)
+            elif t == "jd": ins = g.vector.tensor_tensor(T.jd[:], T.n2[:], T.cq[:], A.subtract)
             elif t == "jh": ins = ts(T.ja[:, 0:64], T.jd[:], 6, None, A.arith_shift_right)
             elif t == "jl": ins = ts(T.ja[:, 64:128], T.jd[:], 63, None, A.bitwise_and)
-            elif t == "jb": ins = g.vector.tensor_copy(T.jb[:], T.ja[:])
-            else: ins = move(e, T.gm[:, 0:8], T.zs[:, 15:128:16])
+            else: ins = ts(cut(T.bk, int(t[2]), 128), T.ja[:], cc["od" if t == "bk1" else "ev"], None, A.mult)
         elif kind == "zw":
-            ins = scaled(e, T["zw%d" % a[0]][:], T.zs[:], col(T.wt, a[0]))
-        elif kind == "zq":
-            ins = scaled(e, T.zq[:, 4 * a[0] + 3:128:16], T.gm[:, 0:8], col(T.wt, a[0]))
+            ins = scaled(e, T["zw%d" % a[0]][:], T.zs[:], col(T.wt, 1 if a[0] == 1 else 32))
         elif kind == "dbl":
             at, n = a
             out, src, b = T.nd[:, at:at + n], T.nd[:, 0:n], col(T.kc, at // 64)
@@ -429,14 +508,13 @@ def rank_program(g, core, T, topo):
         elif kind == "zero":
             ins = g.vector.memset(T.t1[:, 0:P], 0.0)
         elif kind == "fillz":
-            ins = g.sync.dma_start(cut(T.t1, a[0] + 1, G), T.t1[:, 0:P])
+            ins = move(e, cut(T.t1, a[0] + 1, G), T.t1[:, 0:P])
         elif kind == "names":
             ins = g.sync.dma_start(T.t1[0:128:8, :], T.nd[:])
-        elif kind == "block":
-            ins = scaled(e, cut(T.bk, a[0], 128), T.jb[:], col(T.gm, a[0]))
         elif kind == "turn":
-            for j in range(8):
-                ins = g.tensor.matmul(cut(ps, j, 16), T.bk[:, j:G:8], T.b16[:], True, True)
+            for k in range(0, 128, 32):
+                for j in range(8):
+                    ins = g.tensor.matmul(ps[k:k + 32, 16 * j:16 * j + 16], T.bk[k:k + 32, j:256:8], T.b16[k:k + 32, :], True, True)
         elif kind == "turned":
             ins = move(e, cut(T.jt, q, 128), ps[:, 0:128])
         elif kind == "hop0":
@@ -444,19 +522,18 @@ def rank_program(g, core, T, topo):
         elif kind == "jump":
             ins = g.sync.dma_start(T.t1[1:128:8, P + G * a[0]:P + G * (a[0] + 1)], cut(T.jt, a[0], 128))
         elif kind == "ident":
-            ins = g.sync.dma_start(T[a[0]][:, 0:P], T.t1[:, 0:P])
-        elif kind == "sgather":
-            s, k = a
-            if s == 0: ins = move(e, cut(T.gs, k, Q), T.t1[:, 0:P + G * (k + 1)].indirect(mine(T.cd16, k)))
-            else: ins = move(e, cut(T.gs, 2 * s + k, H), T.t1[:].indirect(cut(T.xs, 2 * s + k - 2, 32)))
+            ins = move(e, T[a[0]][:, 0:P], T.t1[:, 0:P])
+        elif kind in ("sgather", "again"):
+            z, s = a
+            x = T.tp16[:, 16 * q:16 * q + 16] if s == 0 else mine(T.cd16, z) if (s == 1 and z < L) else cut(T.xs, 4 * z + s - 1, 16)
+            ins = move(e, cut(T.gs if kind == "sgather" else T.gp, 4 * z + s, Q), T.t1[:, 0:min(W, P + G * (z + 1))].indirect(x))
         elif kind == "spe":
-            ins = compact(ps[:, 0:64], 1, T.gs, a[0] * G, 64)
+            ins = compact(ps[:, 0:16], 1, T.gs, (4 * a[0] + a[1]) * Q, 16)
         elif kind == "sconv":
-            ins = move(e, cut(T.xs, a[0], 64), ps[:, 0:64])
+            ins = move(e, cut(T.xs, 4 * a[0] + a[1], 16), ps[:, 0:16])
         elif kind == "stack":
-            g.tensor.matmul(ps[:, 0:Q], T.eye[:], own(T.t1, a[0]), True, False)
-            for s in range(3):
-                ins = g.tensor.matmul(ps[:, 0:Q], T.dm[:, 2 - s:130 - s], cut(T.gs, 4 * s + a[0], Q), False, s == 2)
+            for s in range(4):
+                ins = g.tensor.matmul(ps[:, 0:Q], shift(s), step(a[0], s), s == 0, s == 3)
         elif kind == "stacked":
             ins = move(e, own(T.t4, a[0]), ps[:, 0:Q])
         elif kind == "hops":
@@ -464,23 +541,25 @@ def rank_program(g, core, T, topo):
         elif kind == "copyu":
             ins = g.sync.dma_start(T["u%d" % a[0]][:, 0:P], T["v%d" % a[0]][:, 0:P])
         elif kind in ("B", "A", "shadow", "vote"):
-            r, l, h = a
+            r, l, c, n = a
             v = T["v%d" % r]
             tab = v if (r == 0 or l == 0) else T["u%d" % r]
-            c0, at = 64 * l + 32 * h, P + G * l + H * h
-            nb = T["tb%d" % r][:, at:at + H]
+            at, x = P + G * l + c, lambda t: t[:, 64 * l + c // 16:64 * l + (c + n) // 16]
+            nb = T["tb%d" % r][:, at:at + n]
             if kind == "B":
-                win = tab[:, 0:P + G * l].indirect(T.fb16[:, c0:c0 + 32])
+                win = tab[:, 0:P + G * l].indirect(x(T.fb16))
                 if e == "V": ins = ts(nb, win, -1.0, 255.0, A.mult, A.add)
                 else: ins = g.scalar.activation(nb, win, F.Identity, bias=255.0, scale=-1.0)
             elif kind == "A":
-                ins = g.vector.tensor_tensor(v[:, at:at + H], tab[:, 0:P + G * l].indirect(T.fa16[:, c0:c0 + 32]), nb, A.min)
+                ins = g.vector.tensor_tensor(v[:, at:at + n], tab[:, 0:P + G * l].indirect(x(T.fa16)), nb, A.min)
             elif kind == "shadow":
-                ins = move(e, nb, v[:, at:at + H])
+                if e == "G": ins = g.affine_select(nb, v[:, at:at + n], [[0, n]], A.is_ge, 0.0, 0, 0)
+                else: ins = move(e, nb, v[:, at:at + n])
             else:
-                ins = g.vector.tensor_tensor(df(r, l, H * h, H * h + H), v[:, 0:at + H].indirect(T.cd16[:, c0:c0 + 32]), nb, A.not_equal)
-        elif kind in ("sum0", "sum1"):
-            for i in range(8 * int(kind[3]), 8 * int(kind[3]) + 8):
+                ins = g.vector.tensor_tensor(df(r, l, c, c + n), v[:, 0:at + n].indirect(x(T.cd16)), nb, A.not_equal)
+        elif kind[:3] == "sum":
+            c, n = parts(*a)[int(kind[3])]
+            for i in range(c // 64, (c + n) // 64):
                 ins = g.tensor.matmul(ps[:, 0:64], T.zs[:, 15 - i:143 - i], df(a[0], a[1], 64 * i, 64 * i + 64), i == 0, i == 15)
         elif kind == "storev":
             ins = g.sync.dma_start(T.yv[:, G * a[0]:G * (a[0] + 1)], T.v2[:, G * a[0]:G * (a[0] + 1)])
@@ -494,31 +573,31 @@ def rank_program(g, core, T, topo):
         elif kind == "totalled":
             ins = move(e, cut(T.dn, a[0] * 4 + a[1], 64), ps[:, 0:64])
         elif kind == "table":
-            ins = g.sync.dma_start(T["tb%d" % a[0]][0:128:16, P + G * a[1]:P + G * (a[1] + 1)], cut(T.dn, a[0] * 4 + a[1], 64))
+            ins = g.sync.dma_start(T["tb%d" % a[0] if a[0] else "t1"][7:128:16, P + G * a[1]:P + G * (a[1] + 1)], cut(T.dn, a[0] * 4 + a[1], 64))
         elif kind[0] in "qp":
             r, l = a[:2]
             z, tb = r * 4 + l, T["tb%d" % r]
-            first = r == 0 and l < 3
-            if kind == "qgather":
-                x = T.tp16[:, 16 * q:16 * q + 16] if r == 0 else mine(T["xl%d" % (r - 1)], l)
-                ins = move(e, cut(T.gq, z, Q), T.t4[:, 0:P + G * (l + 1)].indirect(x))
+            if kind[:5] == "pstep":
+                for s in ((0, 1), (2,), (3,))[int(kind[5])]:
+                    g.tensor.matmul(ps[:, 0:Q], shift(s), step(l + (l == 3), s), s == 0, False)
+                    ins = g.tensor.matmul(ps[:, 0:Q], T.fm[:, 16 - s:144 - s], step(l + (l == 3), s), False, s == 3)
+            elif kind == "pagain":
+                for s in range(4):
+                    ins = g.tensor.matmul(ps[:, 0:Q], T.fm[:, 16 - s:144 - s], cut(T.gp, 4 * l + s, Q) if s else own(T.t1, l), False, s == 3)
+            elif kind == "qgather":
+                ins = move(e, cut(T.gq, z, Q), T.t4[:, 0:P + G * (l + 1)].indirect(mine(T["xl%d" % (r - 1)], l)))
             elif kind == "qpe":
                 for j in range(4):
                     ins = g.tensor.matmul(ps[:, 0:64], T.zq[:, 3 - j:131 - j], T.gq[:, z * Q + j:z * Q + Q:4], j == 0, j == 3)
             elif kind == "qconv": ins = move(e, cut(T.xw, z, 64), ps[:, 0:64])
             elif kind == "pgather":
-                k, win = a[2], tb[:, 0:P + G * (l + 1)]
-                if first: ins = move(e, cut(T.gp, 4 * z + k + 1, Q), win.indirect(cut(T.xs, 4 * k - 4 + l, 16) if k else mine(T.cd16, l)))
-                else: ins = move(e, cut(T.gp, 2 * z + k, H), win.indirect(cut(T.xw, 2 * z + k, 32)))
+                ins = move(e, cut(T.gp, 2 * z + a[2], H), tb[:, 0:P + G * (l + 1)].indirect(cut(T.xw, 2 * z + a[2], 32)))
             elif kind == "prows":
-                ins = g.tensor.matmul(ps[:, 0:Q], T.eye[:], own(T.t4, l) if first else cut(T.gq, z, Q), True, False)
+                ins = g.tensor.matmul(ps[:, 0:Q], T.eye[:], cut(T.gq, z, Q) if r else own(T.t4, l), True, False)
             elif kind == "pflags":
                 for k in range(4):
-                    fk = T.fm[:, 16 - k:144 - k]
-                    if first: ins = g.tensor.matmul(ps[:, 0:Q], fk, cut(T.gp, 4 * z + k, Q) if k else own(tb, l), False, k == 3)
-                    else:
-                        for j in range(4):
-                            ins = g.tensor.matmul(ps[:, j:Q:4], fk, T.gp[:, z * G + 4 * k + j:z * G + G:16], False, k + j == 6)
+                    for j in range(4):
+                        ins = g.tensor.matmul(ps[:, j:Q:4], T.fm[:, 16 - k:144 - k], T.gp[:, z * G + 4 * k + j:z * G + G:16], False, k + j == 6)
             elif kind == "prelu":
                 out = own(T.tb3, l) if (r == RO - 1 and l < 3) else cut(T.gr, z, Q)
                 if e == "V": ins = ts(out, ps[:, 0:Q], 0.0, None, A.max)

import math
from concourse.bass import DstId, RemoteDMATransfer
from concourse.mybir import AluOpType, ActivationFunctionType

N, P, L, G, RO = 4, 1024, 4, 1024, 3
W = P + L * G
Q = G // N
H = G // 2
BIG = 128
EARLY = 2

SCRATCH = {}
for _names, _cols, _dt in (
        ("v0 v1 v2 tb0 tb1 tb2 t1 t4", W, "bfloat16"), ("u1 u2 tb3", 4096, "bfloat16"), ("df gp", 12 * G, "bfloat16"),
        ("gq gr", 12 * Q, "bfloat16"), ("gs", 20 * Q, "bfloat16"), ("gf", 6 * G, "bfloat16"), ("cnt", 12 * 4 * 64, "bfloat16"), ("dn", 12 * 64, "bfloat16"),
        ("nd", 640, "bfloat16"), ("jt", 512, "bfloat16"), ("bk", 256, "bfloat16"), ("one neg zs zw1 zw4 zq dm", 144, "bfloat16"),
        ("fm", 160, "bfloat16"), ("eye", 128, "bfloat16"), ("b16", 16, "bfloat16"), ("fa32 fb32 cd32", 256, "int32"),
        ("tp32 cq nn n2 jd", 64, "int32"), ("ja", 128, "int32"), ("ip ib", 8, "int32"), ("fa16 fb16 cd16 xl0 xl1", 256, "uint16"),
        ("tp16", 64, "uint16"), ("xs", 20 * 16, "uint16"), ("xw", 12 * 64, "uint16"), ("yas ybs", 256, "float32"),
        ("yts xx xk wt", 64, "float32"), ("gm", 32, "float32"), ("cc kc", 16, "float32")):
    for _n in _names.split():
        SCRATCH[_n] = ("sbuf", [128, _cols], _dt)
for _b in range(8):
    SCRATCH["ps%d" % _b] = ("psum", [128, 512], "float32")


def parts(r, l):
    return [(0, H), (H, Q), (H + Q, Q)] if (r == RO - 1 and l >= 2) else [(0, H), (H, H)]


def build_ops():
    ops = {}

    def op(name, kind, eng, cost, n, deps, args=(), bank=None):
        for d in deps:
            assert d in ops, (name, d)
        ops[name] = dict(name=name, kind=kind, eng=eng, cost=cost, n=n, deps=list(deps), args=args, bank=bank)

    def job(names, kinds, sizes, deps, reader, args):
        bank = (names[0], names[-1])
        for k in range(len(names) - 1):
            op(names[k], kinds[k], "P", "pe", sizes[k], deps[k] + names[k - 1:k] * (k > 0), args, bank)
        op(names[-1], kinds[-1], reader, "c1", sizes[-1], [names[-2]] + deps[-1], args, bank)

    op("lx", "load", "Y", "dma", 2048, [], ("x", 0, P))
    for t in ("fb", "fa"):
        op("l%s0" % t, "load", "S", "dma", 256, [], (t, 0, 64))
        op("l%s1" % t, "load", "Y", "dma", 768, [], (t, 64, 256))
        op("c%s0" % t, "conv", "V", "c1", 64, ["l%s0" % t], (t, 0, 64))
        op("c%s1" % t, "conv", "V", "c1", 192, ["l%s1" % t], (t, 64, 256))
    op("lcq", "loadq", "Y", "dma", 256, [])
    op("lcd", "load", "S", "dma", 1024, [], ("cd", 0, 256))
    op("ccd0", "conv", "V", "c1", 64, ["lcd"], ("cd", 0, 64))
    op("ccd1", "conv", "V", "c1", 192, ["lcd"], ("cd", 64, 256))
    op("ltp", "load", "Y", "dma", 256, [], ("tp", 0, 64))
    op("ctp", "conv", "V", "c1", 64, ["ltp"], ("tp", 0, 64))
    lst = lambda t, l: "c%s%d" % (t, min(l, 1))
    for t, n, d in (("ip", 1, []), ("xx", 64, []), ("nn", 64, []), ("one", 144, []), ("zs0", 144, ["one"]), ("zs", 144, ["zs0"]),
                    ("eye", 128, ["one"]), ("dm", 136, ["one"]), ("neg", 144, []), ("fm0", 144, ["neg"]), ("fm", 144, ["fm0"]),
                    ("zq0", 144, []), ("xk", 64, []), ("gm0", 32, ["one"]), ("gm", 32, ["gm0"])):
        op(t, "pool", "G", "pool", n, d, (t,))
    for t, n, d in (("ib", 1, ["ip"]), ("i8", 1, ["ip"]), ("od", 1, ["ip"]), ("bf", 3, ["ib", "i8", "od"]), ("ev", 1, ["od"]),
                    ("al", 1, ["ib"]), ("be", 1, ["ib"]), ("ga", 1, ["ib", "al"]), ("kc", 9, ["al", "xx"]),
                    ("nd0", 64, ["be", "ga", "xx"]), ("b16", 16, ["bf", "xx"]), ("n2", 64, ["bf", "nn"]), ("ws", 1, ["al"]),
                    ("w0", 1, ["i8"]), ("wk", 40, ["bf", "xk"]), ("wt", 40, ["ws", "w0", "wk"]), ("zq", 32, ["zq0", "gm", "wt"]),
                    ("jd", 64, ["n2", "lcq"]), ("jh", 64, ["jd"]), ("jl", 64, ["jd"]), ("bk0", 128, ["jh", "jl", "ev"]),
                    ("bk1", 128, ["jh", "jl", "bf"])):
        op(t, "tiny", "V", "c1", n, d, (t,))
    for k in (1, 4):
        op("zw%d" % k, "zw", "VS", "ch", 144, ["zs", "wt"], (k,))
    for k, (at, n) in enumerate(((64, 64), (128, 128), (256, 256), (512, 128))):
        op("nd%d" % (k + 1), "dbl", "VS", "ch", n, ["nd%d" % min(k, 2), "kc"], (at, n))
    op("zero", "zero", "V", "ch", P, [])
    for l in range(L):
        op("fz%d" % l, "fillz", "SY", "cp", G, ["zero"], (l,))
    op("tn", "names", "Y", "dma", 1280, ["nd3", "nd4"] + ["fz%d" % l for l in range(L)])
    job(["turn", "jt"], ["turn", "turned"], [32 * 32, 128], [["bk0", "bk1", "b16"], []], "VS", ())
    op("h0_", "hop0", "G", "hop", 256, ["jt"])
    for l in range(L):
        op("tj%d" % l, "jump", "Y", "dma", 256, ["jt", "h0_", "fz%d" % l], (l,))
    op("it4", "ident", "YS", "cp", G, ["tn"], ("t4",))
    op("it3", "ident", "YS", "cp", G, ["tn"], ("tb3",))

    def follow(z, steps, tab, x):
        for s in steps:
            op("sg%d%d" % (z, s), "sgather", "VS", "g", Q, tab + [x], (z, s))
            if s < 3:
                x = "sc%d%d" % (z, s)
                job(["sp%d%d" % (z, s), x], ["spe", "sconv"], [16 * 64, 16], [["sg%d%d" % (z, s), "zw1"], []], "V", (z, s))
        if z < L:
            job(["st%d" % z, "sq%d" % z], ["stack", "stacked"], [4 * Q, Q], [["sg%d3" % z, "eye", "dm"], []], "VS", (z,))
            op("hs%d" % z, "hops", "G", "hop", 512, ["sq%d" % z], (z,))

    for l in range(EARLY):
        follow(l, (1, 2, 3), ["tn"] + ["tj%d" % k for k in range(l + 1)], lst("cd", l))

    for r in range(RO):
        inp = ["lx"] if r == 0 else ["np%d_0" % (r - 1), "np%d_1" % (r - 1)]
        if r > 0:
            op("iu%d" % r, "copyu", "Y", "dma", 2048, inp, (r,))
        src = list(inp)
        for l in range(L):
            rl, a = "%d%d" % (r, l), (r, l)
            low = inp + ["A%d%d%d" % (r, k, h) for k in range(l) for h in range(len(parts(r, k)))]
            both = ["A%s%d" % (rl, h) for h in range(len(parts(r, l)))]
            for h, (c, n) in enumerate(parts(r, l)):
                op("B%s%d" % (rl, h), "B", "VS", "g", n, src + [lst("fb", l)], (r, l, c, n))
                op("A%s%d" % (rl, h), "A", "V", "g", n, src + [lst("fa", l), "B%s%d" % (rl, h)], (r, l, c, n))
                op("cp%s%d" % (rl, h), "shadow", "YGVS", "cp", n, ["A%s%d" % (rl, h)], (r, l, c, n))
                op("vo%s%d" % (rl, h), "vote", "V", "g", n, low + both[:h + 1] + ["cp%s%d" % (rl, h), lst("cd", l)], (r, l, c, n))
            if r == RO - 1:
                if l == 0:
                    op("sv0", "storev", "Y", "dma", 2048, inp, (0,))
                op("sv%d" % (l + 1), "storev", "Y", "dma", 2048, both, (l + 1,))
            job(["su%s%d" % (rl, h) for h in range(len(both))] + ["cn" + rl], ["sum%d" % h for h in range(len(both))] + ["count"],
                [n for c, n in parts(r, l)] + [64], [["vo%s%d" % (rl, h), "zs"] for h in range(len(both))] + [[]], "VS", a)
            op("h1_" + rl, "hop1", "G", "hop", 128, ["cn" + rl], a)
            job(["ex" + rl, "mi" + rl], ["total", "totalled"], [4 * 64, 64], [["cn" + rl, "h1_" + rl, "eye"], []], "VS", a)
            op("tw" + rl, "table", "Y", "dma", 128, ["mi" + rl] + (["tn", "tj%d" % l] + ["sg%d3" % k for k in range(l, EARLY)] + ["st%d" % l] * (l < EARLY)) * (r == 0), a)
            tab = ["tw%d%d" % (r, k) for k in range(l + 1)]
            if r == 0 and l < EARLY:
                for s in (1, 2, 3):
                    op("pg%s%d" % (rl, s), "again", "VS", "g", Q, tab + ["sg%d%d" % (l, s)], (l, s))
                job(["pa" + rl, "pb" + rl, "pr" + rl], ["prows", "pagain", "prelu"], [Q, 4 * Q, Q],
                    [["sq%d" % l], ["pg%s%d" % (rl, s) for s in (1, 2, 3)] + ["fm"], []], "VS", a)
            elif r == 0:
                follow(l, (1, 2, 3), tab, lst("cd", l))
                z = l + (l == 3)
                if l == 3: follow(z, (0, 1, 2, 3), tab, "ctp")
                job(["pa" + rl, "pb" + rl, "pc" + rl, "pr" + rl], ["pstep0", "pstep1", "pstep2", "prelu"], [4 * Q, 2 * Q, 2 * Q, Q],
                    [["sg%d1" % z, "eye", "dm", "fm"], ["sg%d2" % z], ["sg%d3" % z], []], "VS", a)
            else:
                op("qg" + rl, "qgather", "VS", "g", Q,
                   ["it4", "pl%d%d" % (r - 1, l)] + [t + str(k) for k in range(l + 1) for t in ("sq", "hs")], a)
                job(["qa" + rl, "qc" + rl], ["qpe", "qconv"], [4 * 64, 64], [["qg" + rl, "zq"], []], "V", a)
                for k in range(2):
                    op("pg%s%d" % (rl, k), "pgather", "VS", "g", H, tab + ["cn%d0" % (r - 1), "qc" + rl], (r, l, k))
                job(["pa" + rl, "pb" + rl, "pr" + rl], ["prows", "pflags", "prelu"], [Q, 4 * Q, Q],
                    [["qg" + rl, "eye"], ["pg%s0" % rl, "pg%s1" % rl, "fm"], ["it3"] * (r == RO - 1 and l < 3)], "VS", a)
            x = "pr" + rl
            if r < RO - 1 or l == 3:
                x = "pl" + rl
                job(["pp" + rl, x], ["ppe", "pconv"], [16 * 64, 16], [["pr" + rl, "zw4"], []], "VS" if r == RO - 1 else "V", a)
            if not (r == 1 and l == 3):
                op("h3_" + rl, "hop3", "G", "hop", 512 if (r == RO - 1 and l < 3) else 32, [x], a)
            if r == 0 or l == L - 1:
                src = src + both
            else:
                for h in range(2):
                    op("u%s%d" % (rl, h), "u", "VS", "g", H,
                       low + (both if h else both[:1]) + ["h3_%d%d" % (r - 1, l), "pl%d%d" % (r - 1, l)], (r, l, h))
                src = ["iu%d" % r] + ["u%d%d%d" % (r, k, h) for k in range(l + 1) for h in range(2)]
        if r < RO - 1:
            allv = low + both
            for h in range(2):
                op("np%d_%d" % (r, h), "np", "VS", "g", H, allv + (["ctp"] if r == 0 else ["h3_03", "pl03"]), (r, h))
    op("syt", "storet", "Y", "dma", 256, ["h3_23", "pl23"])
    for t in ("fa", "fb"):
        op("y0" + t, "y0", "V", "c1", 64, ["l%s0" % t], (t,))
        for l in range(1, L):
            tab = ["it3"] + ["h3_2%d" % k for k in range(l)] + ["pr2%d" % k for k in range(l)]
            for h in range(2):
                op("fg%s%d%d" % (t, l, h), "fgather", "VS", "g", H, tab + [lst(t, l)], (t, l, h))
            job(["fp%s%d" % (t, l), "fc%s%d" % (t, l)], ["fpe", "fcopy"], [16 * 64, 64],
                [["fg%s%d0" % (t, l), "fg%s%d1" % (t, l), "zw4"], []], "VS", (t, l))
        op("sy%s0" % t, "storey", "Y", "dma", 768, ["y0" + t, "fc%s1" % t, "fc%s2" % t], (t, 0, 192))
        op("sy%s1" % t, "storey", "YS", "dma", 256, ["fc%s3" % t], (t, 192, 256))
    return ops


OPS = build_ops()
SEMAPHORES = ["cV", "cS", "cP", "cG", "sent"] + ["s_" + n for n, o in OPS.items() if o["cost"] in ("dma", "hop", "cp")]

GUESSES = [dict(zip("cycle gather pe call sem issue start rissue rstart row byte first".split(), v)) for v in (
    (0.00096, 0.0014, 0.00055, 0.0, 0.09, 0.25, 0.85, 0.2, 1.4, 0.024, 0.000035, 0.5),
    (0.001, 0.0012, 0.0005, 0.02, 0.07, 0.4, 1.0, 0.9, 1.5, 0.035, 0.00003, 2.5),
    (0.0009, 0.0011, 0.0005, 0.02, 0.13, 0.3, 1.3, 0.4, 0.7, 0.012, 0.00004, 1.2))]
QUEUES = "VSPGY"
OPENING = "lx lfb0 lcq lfa0 lcd lfb1 lfa1".split()
LEAN, SWEEPS, STEPS, HEAT = 0.8, 6, 320000, 0.004


def needs(o, e, m):
    c, n = o["cost"], o["n"]
    if c == "dma" or (c == "cp" and e == "Y"): return m["issue"], m["start"], 8 * (m["row"] + n * m["byte"] * (2 if c == "cp" else 1))
    if c == "hop": return m["rissue"], m["rstart"], 32 * (m["row"] + n * m["byte"])
    if c == "g": return 0.055 + n * m["gather"], 0, 0
    if c == "pe": return n * m["pe"], 0, 0
    if e == "G": return 0.16 + 2 * n * m["cycle"], 0, 0
    return m["call"] + max(64, n // 2 if (c in ("ch", "cp") and e == "V") else n) * m["cycle"], 0, 0


def sweep(rank, before, back):
    busy = {e: [] for e in "VSPGYD"}
    start, end, eng = {}, {}, {}
    todo = sorted(OPS, key=lambda n: rank[n])
    while todo:
        n = next(x for x in todo if all(d in end for d in before[x]))
        todo.remove(n)
        best = None
        for e in OPS[n]["eng"][:2]:
            hold, off, d = needs(OPS[n], e, GUESSES[0])
            t = off + d if d else hold
            use = [(e, t - hold if back else 0.0, hold)] + [("D", 0.0 if back else off, d)] * (d > 0)
            s, moved = max([end[x] + GUESSES[0]["sem"] for x in before[n]] + [0.0]), True
            while moved:
                moved = False
                for res, o, w in use:
                    for a, b in busy[res]:
                        if a < s + o + w - 1e-9 and s + o < b - 1e-9: s, moved = b - o, True
            key = s + t + (LEAN if e == "V" else 0.0)
            if best is None or key < best[0]: best = (key, s, t, e, use)
        key, s, t, e, use = best
        for res, o, w in use:
            busy[res].append((s + o, s + o + w))
            busy[res].sort()
        start[n], end[n], eng[n] = s, s + t, e
    return start, end, eng


def with_banks(order, eng):
    free, bank, extra = [(b, None) for b in range(8)], {}, {}
    for n in order:
        if OPS[n]["bank"]:
            job, reader = OPS[n]["bank"]
            if n == job:
                if not free: return None
                bank[job], last = free.pop(0)
                if last: extra[n] = last
            if n == reader: free.append((bank[job], n))
    return order, eng, bank, extra


def behind(order, eng, users, cost, m, run, old, same):
    rest, issue, nxt, dma, sem = list(old[3]), list(old[5]), [0.0] * 5, 0.0, m["sem"]
    for n in order[same + 60:same:-1]:
        nxt[eng[n]] = issue[n] - sem
        if cost[n][eng[n]][2]: dma = rest[n] + cost[n][eng[n]][2]
    for n in order[same::-1]:
        e = eng[n]
        hold, off, d = cost[n][e]
        t = dma if d else 0.0
        for x in users[n]:
            if issue[x] > t: t = issue[x]
        rest[n] = t
        if d: dma = t = t + d
        t += off if d else hold
        if hold + nxt[e] > t: t = hold + nxt[e]
        nxt[e], issue[n] = t, t + sem
    n, pairs, why = run[0].index(max(run[0])), [], run[1]
    while n is not None:
        if why[n][1] and why[n][0] is not None: pairs.append((why[n][0], n))
        n = why[n][0]
    return run + (rest, pairs, issue)


def replay(order, eng, extra, deps, cost, m, old, at, same, bound, used):
    at -= at % 16
    done, why, marks = list(old[0]), list(old[1]), old[2][:at // 16 + 1]
    free, last, dma, first = marks[-1]
    free, last, sem, was, rest, reach = list(free), list(last), m["sem"], old[0], old[3], max(same, used[0])
    for i in range(at, len(order)):
        n = order[i]
        if i % 16 == 0 and i > at:
            marks.append((tuple(free), tuple(last), dma, first))
            if i > reach and marks[-1] == old[2][i // 16]: return done, why, marks + old[2][i // 16 + 1:]
        e = eng[n]
        t, w, queued = free[e], last[e], True
        for d in deps[n] + [extra[n]] if n in extra else deps[n]:
            if done[d] + sem > t: t, w, queued = done[d] + sem, d, False
        hold, off, d = cost[n][e]
        if d:
            if e == 3: t, first = t + first, 0.0
            if dma > t + off: w, queued = last[5], True
            else: dma = t + off
            dma = done[n] = dma + d
            last[5] = n
        else: done[n] = t + hold
        if done[n] != was[n]:
            if i > same and done[n] + rest[n] > bound: return None
            if used[n] > reach: reach = used[n]
        free[e], last[e], why[n] = t + hold, n, (w, queued)
    return done, why, marks


def make_plan():
    before = {n: o["deps"] for n, o in OPS.items()}
    after = {n: [x for x in OPS if n in before[x]] for n in OPS}
    names = list(OPS)
    index = {n: i for i, n in enumerate(names)}
    start, end, eng = sweep(index, before, False)
    for k in range(SWEEPS):
        start, end, eng = sweep({n: -end[n] for n in OPS}, after, True)
        start, end, eng = sweep({n: -end[n] for n in OPS}, before, False)
    below = {}
    for n in OPS:
        below[n] = set(before[n]).union(*[below[d] for d in before[n]])
    deps = [[index[d] for d in dict.fromkeys(before[n]) if not any(d in below[x] for x in before[n])] for n in names]
    users = [[i for i, d in enumerate(deps) if k in d] for k in range(len(names))]
    may = [[QUEUES.index(e) for e in OPS[n]["eng"]] for n in names]
    costs = [[[needs(OPS[n], e, m) if e in OPS[n]["eng"] else None for e in QUEUES] for n in names] for m in GUESSES]
    role = [OPS[n]["bank"].index(n) + 1 if n in (OPS[n]["bank"] or ()) else 0 for n in names]
    state = [12345]

    def draw(k):
        state[0] = (state[0] * 1103515245 + 12345) % 2 ** 31
        return (state[0] >> 8) % k

    def waits(order):
        free, extra = [None] * 8, {}
        for n in order:
            if role[n] == 2: free.append(n)
            elif role[n]:
                if not free: return None
                if free[0] is not None: extra[n] = free[0]
                del free[0]
        return extra

    def last_use(order, extra):
        used = [0] * len(order)
        for i, n in enumerate(order):
            for d in deps[n]: used[d] = i
            if n in extra: used[extra[n]] = i
        return used

    order = [index[n] for n in OPENING + sorted(set(OPS) - set(OPENING), key=lambda n: (start[n], index[n]))]
    eng = [QUEUES.index(eng[n]) for n in names]
    zeros = [0.0] * len(names)
    empty = lambda m: (zeros, [None] * len(names), [([0.0] * 5, [None] * 6, 0.0, m["first"])], zeros, [], zeros)
    runs = [behind(order, eng, users, c, m, replay(order, eng, waits(order), deps, c, m, empty(m), 0, len(order), 0, zeros), empty(m), len(order))
            for c, m in zip(costs, GUESSES)]
    scale = [1.0 / max(x[0]) for x in runs]
    now = [1.0] * len(runs)
    best, held = (sum(now), order, eng), waits(order)
    used, never = last_use(order, held), [len(order)] * len(order)
    for step in range(STEPS):
        pairs = runs[draw(len(runs))][4]
        a, b = pairs[draw(len(pairs))]
        order2, eng2, how = order, eng, draw(10)
        if how < 3:
            n = (a, b, order[draw(len(order))])[how]
            eng2 = list(eng)
            eng2[n] = may[n][draw(len(may[n]))]
            if eng2[n] == eng[n]: continue
            i = j = order.index(n)
        else:
            far = (0, 0, 4, 10, 25, 60)[draw(6)]
            i, j = order.index(a), order.index(b)
            if how < 7: i, keep, links, part = i - far, {b}, deps, order[max(0, i - far):j + 1][::-1]
            else: j, keep, links, part = j + far, {a}, users, order[i:j + far + 1]
            for n in part:
                if n in keep: keep.update(links[n])
            if i < len(OPENING) or (a in keep and b in keep): continue
            order2 = order[:i] + sorted(order[i:j + 1], key=lambda n: (n in keep) != (how < 7)) + order[j + 1:]
        extra = waits(order2) if how > 2 and any(role[n] for n in keep) else held
        if extra is None: continue
        limit = sum(now) - HEAT * 0.1 ** (step / STEPS) * math.log((draw(10000) + 1) / 10001.0)
        tried, new = [], []
        for k in range(len(runs)):
            room = limit - sum(new) - sum(now[k + 1:]) + 0.004 * (len(runs) - 1 - k)
            tried.append(replay(order2, eng2, extra, deps, costs[k], GUESSES[k], runs[k], i, j, room / scale[k],
                                used if extra == held else never))
            if tried[k] is None: break
            new.append(max(tried[k][0]) * scale[k])
        if len(new) == len(runs) and sum(new) <= limit:
            if order2 is not order: used = last_use(order2, extra)
            now, order, eng, held = new, order2, eng2, extra
            runs = [behind(order, eng, users, c, m, x, y, j) for c, m, x, y in zip(costs, GUESSES, tried, runs)]
            if sum(now) < best[0]: best = (sum(now), order, eng)
    return with_banks([names[n] for n in best[1]], {n: QUEUES[best[2][index[n]]] for n in names})


PLAN = make_plan()


def engine_masks(topo, cores, src):
    far = [c for c in cores if topo.chip(c) != topo.chip(src)]
    near = [c for c in cores if c != src and topo.chip(c) == topo.chip(src)]
    out, used = {}, set()
    for group in (far, near):
        for i, c in enumerate(group):
            es = [e for e in topo.engines(src, c) if e not in used]
            k = len(es) // len(group)
            out[c] = es[i * k:(i + 1) * k]
        used |= set(e for c in group for e in out[c])
    return out


def rank_program(g, core, T, topo):
    q = T.rank_of(core)
    if q is None:
        return
    order, eng, bank, extra = PLAN
    cores = [int(c) for c in T.cores]
    masks = {c: engine_masks(topo, cores, c) for c in cores}
    arrive = sum(len(masks[c][core]) for c in cores if c != core)
    leave = sum(len(v) for v in masks[core].values())
    queue = {"V": g.vector, "S": g.scalar, "P": g.tensor, "G": g, "Y": g.sync}
    A, F = AluOpType, ActivationFunctionType
    count = {e: 0 for e in "VSPG"}
    mark = {}
    seen = {e: {} for e in queue}
    sent = [0]

    def wait(e, names):
        need = {}
        for a in names:
            s, k = mark[a]
            need[s] = max(need.get(s, 0), k)
        for s, k in need.items():
            if seen[e].get(s, 0) < k:
                queue[e].wait_ge(T.sem[s], k)
                seen[e][s] = k

    def move(e, out, src):
        if e == "V": return g.vector.tensor_copy(out, src)
        if e == "S": return g.scalar.activation(out, src, F.Copy)
        return g.sync.dma_start(out, src)

    def scaled(e, out, src, m):
        if e == "V": return g.vector.tensor_scalar(out, src, m, None, A.mult)
        return g.scalar.activation(out, src, F.Identity, scale=m)

    def spread(name, part):
        tr = []
        for p in range(N):
            if p == q: continue
            rid, pid, se = topo.addr(cores[p])
            m = sum(1 << e for e in masks[core][cores[p]])
            tr.append(RemoteDMATransfer(dst_ids=[DstId(rid=rid, pnc=pid)], dma_engine_mask=m, remote_sem=T.sem["s_" + name],
                                        src=part, dst=part))
        g.remote_dma_fused(tr, local_sem=T.sem.sent)
        sent[0] += leave

    def compact(out, k, buf, a, n):
        for i in range(16):
            ins = g.tensor.matmul(out, T["zw%d" % k][:, 15 - i:143 - i], buf[:, a + i:a + 16 * n:16], i == 0, i == 15)
        return ins

    col = lambda t, j: t[:, j:j + 1]
    cut = lambda t, k, n, m=1: t[:, k * n:(k + m) * n]
    cc = {k: col(T.cc, j) for j, k in enumerate(("bf", "mf", "od", "ev", "al", "be", "ga", "ws", "w0"))}
    own = lambda t, l: t[:, P + G * l + Q * q:P + G * l + Q * q + Q]
    mine = lambda t, l: t[:, 64 * l + 16 * q:64 * l + 16 * q + 16]
    step = lambda z, s: own(T.t1, z) if (s == 0 and z < L) else cut(T.gs, 4 * z + s, Q)
    shift = lambda s: T.dm[:, 3 - s:131 - s] if s else T.eye[:]
    cnt = lambda r, l, p: cut(T.cnt, (r * 4 + l) * 4 + p, 64)
    df = lambda r, l, a, b: T["tb%d" % (r + 1)][:, a:b] if (l == 0 and r < RO - 1) else T.df[:, (r * 4 + l) * G + a:(r * 4 + l) * G + b]

    for name in order:
        o, e = OPS[name], eng[name]
        kind, a = o["kind"], o["args"]
        wait(e, [d for d in o["deps"] if not (e == "P" and OPS[d]["bank"] == o["bank"])] + ([extra[name]] if name in extra else []))
        ps = T["ps%d" % bank[o["bank"][0]]] if o["bank"] else None
        ts, ib = g.vector.tensor_scalar, col(T.ib, 0)
        ins = None
        if kind == "load":
            ins = queue[e].dma_start((T.v0 if a[0] == "x" else T[a[0] + "32"])[:, a[1]:a[2]], T[a[0]][:, a[1]:a[2]])
        elif kind == "loadq":
            ins = queue[e].dma_start(T.cq[:], cut(T.cd, q, 64))
        elif kind == "conv":
            ins = g.vector.tensor_copy(T[a[0] + "16"][:, a[1]:a[2]], T[a[0] + "32"][:, a[1]:a[2]])
        elif kind == "pool":
            t, small = a[0], dict(allow_small_or_imprecise_dtypes=True)
            if t == "ip": ins = g.iota(col(T.ip, 0), [[0, 1]], 0, 1)
            elif t == "xx": ins = g.iota(T.xx[:], [[1, 64]], 0, 0, **small)
            elif t == "nn": ins = g.iota(T.nn[:], [[16, 64]], P + G * q, 0)
            elif t in ("one", "neg", "zq0"): ins = g.iota(T[t[:2 + (t != "zq0")]][:], [[0, 144]], {"one": 1, "neg": -BIG, "zq0": 0}[t], 0, **small)
            elif t == "xk": ins = g.iota(T.xk[:], [[4, 2], [0, 8], [1, 4]], 0, 0, **small)
            elif t == "gm0": ins = g.affine_select(T.gm[:], T.one[:, 0:32], [[-16, 8], [0, 4]], A.is_ge, 0.0, 0, 1)
            elif t == "gm": ins = g.affine_select(T.gm[:], T.gm[:], [[16, 8], [0, 4]], A.is_ge, 0.0, 15, -1)
            elif t == "zs0": ins = g.affine_select(T.zs[:], T.one[:], [[-16, 9], [1000, 16]], A.is_ge, 0.0, -15000, 1)
            elif t == "zs": ins = g.affine_select(T.zs[:], T.zs[:], [[16, 9], [0, 16]], A.is_ge, 0.0, 15, -1)
            elif t == "eye": ins = g.affine_select(T.eye[:], T.one[:, 0:128], [[-1, 128]], A.is_equal, 0.0, 0, 1)
            elif t == "dm": ins = g.affine_select(T.dm[:, 0:136], T.one[:, 0:136], [[-8, 17], [1000, 8]], A.is_equal, 0.0, -4001, 1)
            elif t == "fm0": ins = g.affine_select(T.fm[:, 1:145], T.neg[:], [[-16, 9], [0, 16]], A.is_equal, 0.0, 9, 1)
            else: ins = g.affine_select(T.fm[:, 1:145], T.fm[:, 1:145], [[0, 18], [1, 2], [0, 4]], A.is_equal, 0.0, 0, 0)
        elif kind == "tiny":
            t = a[0]
            if t == "ib": ins = ts(ib, col(T.ip, 0), 15, None, A.bitwise_and)
            elif t == "i8": ins = ts(col(T.ib, 1), col(T.ip, 0), 7, None, A.bitwise_and)
            elif t == "od": ins = ts(col(T.ib, 2), col(T.ip, 0), 4, 1, A.arith_shift_right, A.bitwise_and)
            elif t == "bf": ins = g.vector.tensor_copy(T.cc[:, 0:3], T.ib[:, 0:3])
            elif t == "ev": ins = ts(cc["ev"], col(T.ib, 2), 0.0, None, A.is_equal)
            elif t == "al": ins = ts(cc["al"], ib, 8.0, None, A.is_lt)
            elif t == "be": ins = ts(cc["be"], ib, 8.0, None, A.is_ge)
            elif t == "ga": ins = ts(cc["ga"], ib, 10.0, cc["al"], A.mult, A.mult)
            elif t == "kc": ins = ts(T.kc[:, 0:9], T.xx[:, 0:9], cc["al"], None, A.mult)
            elif t == "nd0": ins = ts(T.nd[:, 0:64], T.xx[:, 0:64], cc["be"], cc["ga"], A.mult, A.add)
            elif t == "b16": ins = ts(T.b16[:], T.xx[:, 0:16], cc["bf"], None, A.is_equal)
            elif t == "n2": ins = ts(T.n2[:], T.nn[:], cc["bf"], None, A.add)
            elif t == "ws": ins = ts(cc["ws"], cc["al"], 63.0, 1.0, A.mult, A.add)
            elif t == "w0": ins = ts(cc["w0"], col(T.ib, 1), 0.0, 2.0, A.is_equal, A.mult)
            elif t == "wk": ins = ts(T.wt[:, 0:33], T.xk[:, 0:33], cc["mf"], -1.0, A.is_ge, A.mult)
            elif t == "wt": ins = ts(T.wt[:, 0:33], T.wt[:, 0:33], cc["w0"], cc["ws"], A.add, A.mult)
            elif t == "zq": ins = g.vector.tensor_tensor(T.zq[:, 3:128:4], T.gm[:], T.wt[:, 0:32], A.mult)
            elif t == "jd": ins = g.vector.tensor_tensor(T.jd[:], T.n2[:], T.cq[:], A.subtract)
            elif t == "jh": ins = ts(T.ja[:, 0:64], T.jd[:], 6, None, A.arith_shift_right)
            elif t == "jl": ins = ts(T.ja[:, 64:128], T.jd[:], 63, None, A.bitwise_and)
            else: ins = ts(cut(T.bk, int(t[2]), 128), T.ja[:], cc["od" if t == "bk1" else "ev"], None, A.mult)
        elif kind == "zw":
            ins = scaled(e, T["zw%d" % a[0]][:], T.zs[:], col(T.wt, 1 if a[0] == 1 else 32))
        elif kind == "dbl":
            at, n = a
            out, src, b = T.nd[:, at:at + n], T.nd[:, 0:n], col(T.kc, at // 64)
            if e == "V": ins = ts(out, src, b, None, A.add)
            else: ins = g.scalar.activation(out, src, F.Identity, bias=b)
        elif kind == "zero":
            ins = g.vector.memset(T.t1[:, 0:P], 0.0)
        elif kind == "fillz":
            ins = move(e, cut(T.t1, a[0] + 1, G), T.t1[:, 0:P])
        elif kind == "names":
            ins = g.sync.dma_start(T.t1[0:128:8, :], T.nd[:])
        elif kind == "turn":
            for k in range(0, 128, 32):
                for j in range(8):
                    ins = g.tensor.matmul(ps[k:k + 32, 16 * j:16 * j + 16], T.bk[k:k + 32, j:256:8], T.b16[k:k + 32, :], True, True)
        elif kind == "turned":
            ins = move(e, cut(T.jt, q, 128), ps[:, 0:128])
        elif kind == "hop0":
            spread(name, cut(T.jt, q, 128))
        elif kind == "jump":
            ins = g.sync.dma_start(T.t1[1:128:8, P + G * a[0]:P + G * (a[0] + 1)], cut(T.jt, a[0], 128))
        elif kind == "ident":
            ins = move(e, T[a[0]][:, 0:P], T.t1[:, 0:P])
        elif kind in ("sgather", "again"):
            z, s = a
            x = T.tp16[:, 16 * q:16 * q + 16] if s == 0 else mine(T.cd16, z) if (s == 1 and z < L) else cut(T.xs, 4 * z + s - 1, 16)
            ins = move(e, cut(T.gs if kind == "sgather" else T.gp, 4 * z + s, Q), T.t1[:, 0:min(W, P + G * (z + 1))].indirect(x))
        elif kind == "spe":
            ins = compact(ps[:, 0:16], 1, T.gs, (4 * a[0] + a[1]) * Q, 16)
        elif kind == "sconv":
            ins = move(e, cut(T.xs, 4 * a[0] + a[1], 16), ps[:, 0:16])
        elif kind == "stack":
            for s in range(4):
                ins = g.tensor.matmul(ps[:, 0:Q], shift(s), step(a[0], s), s == 0, s == 3)
        elif kind == "stacked":
            ins = move(e, own(T.t4, a[0]), ps[:, 0:Q])
        elif kind == "hops":
            spread(name, own(T.t4, a[0]))
        elif kind == "copyu":
            ins = g.sync.dma_start(T["u%d" % a[0]][:, 0:P], T["v%d" % a[0]][:, 0:P])
        elif kind in ("B", "A", "shadow", "vote"):
            r, l, c, n = a
            v = T["v%d" % r]
            tab = v if (r == 0 or l == 0) else T["u%d" % r]
            at, x = P + G * l + c, lambda t: t[:, 64 * l + c // 16:64 * l + (c + n) // 16]
            nb = T["tb%d" % r][:, at:at + n]
            if kind == "B":
                win = tab[:, 0:P + G * l].indirect(x(T.fb16))
                if e == "V": ins = ts(nb, win, -1.0, 255.0, A.mult, A.add)
                else: ins = g.scalar.activation(nb, win, F.Identity, bias=255.0, scale=-1.0)
            elif kind == "A":
                ins = g.vector.tensor_tensor(v[:, at:at + n], tab[:, 0:P + G * l].indirect(x(T.fa16)), nb, A.min)
            elif kind == "shadow":
                if e == "G": ins = g.affine_select(nb, v[:, at:at + n], [[0, n]], A.is_ge, 0.0, 0, 0)
                else: ins = move(e, nb, v[:, at:at + n])
            else:
                ins = g.vector.tensor_tensor(df(r, l, c, c + n), v[:, 0:at + n].indirect(x(T.cd16)), nb, A.not_equal)
        elif kind[:3] == "sum":
            c, n = parts(*a)[int(kind[3])]
            for i in range(c // 64, (c + n) // 64):
                ins = g.tensor.matmul(ps[:, 0:64], T.zs[:, 15 - i:143 - i], df(a[0], a[1], 64 * i, 64 * i + 64), i == 0, i == 15)
        elif kind == "storev":
            ins = g.sync.dma_start(T.yv[:, G * a[0]:G * (a[0] + 1)], T.v2[:, G * a[0]:G * (a[0] + 1)])
        elif kind == "count":
            ins = move(e, cnt(a[0], a[1], q), ps[:, 0:64])
        elif kind == "hop1":
            spread(name, cnt(a[0], a[1], q))
        elif kind == "total":
            for p in range(N):
                ins = g.tensor.matmul(ps[:, 0:64], T.eye[:], cnt(a[0], a[1], p), p == 0, p == N - 1)
        elif kind == "totalled":
            ins = move(e, cut(T.dn, a[0] * 4 + a[1], 64), ps[:, 0:64])
        elif kind == "table":
            ins = g.sync.dma_start(T["tb%d" % a[0] if a[0] else "t1"][7:128:16, P + G * a[1]:P + G * (a[1] + 1)], cut(T.dn, a[0] * 4 + a[1], 64))
        elif kind[0] in "qp":
            r, l = a[:2]
            z, tb = r * 4 + l, T["tb%d" % r]
            if kind[:5] == "pstep":
                for s in ((0, 1), (2,), (3,))[int(kind[5])]:
                    g.tensor.matmul(ps[:, 0:Q], shift(s), step(l + (l == 3), s), s == 0, False)
                    ins = g.tensor.matmul(ps[:, 0:Q], T.fm[:, 16 - s:144 - s], step(l + (l == 3), s), False, s == 3)
            elif kind == "pagain":
                for s in range(4):
                    ins = g.tensor.matmul(ps[:, 0:Q], T.fm[:, 16 - s:144 - s], cut(T.gp, 4 * l + s, Q) if s else own(T.t1, l), False, s == 3)
            elif kind == "qgather":
                ins = move(e, cut(T.gq, z, Q), T.t4[:, 0:P + G * (l + 1)].indirect(mine(T["xl%d" % (r - 1)], l)))
            elif kind == "qpe":
                for j in range(4):
                    ins = g.tensor.matmul(ps[:, 0:64], T.zq[:, 3 - j:131 - j], T.gq[:, z * Q + j:z * Q + Q:4], j == 0, j == 3)
            elif kind == "qconv": ins = move(e, cut(T.xw, z, 64), ps[:, 0:64])
            elif kind == "pgather":
                ins = move(e, cut(T.gp, 2 * z + a[2], H), tb[:, 0:P + G * (l + 1)].indirect(cut(T.xw, 2 * z + a[2], 32)))
            elif kind == "prows":
                ins = g.tensor.matmul(ps[:, 0:Q], T.eye[:], cut(T.gq, z, Q) if r else own(T.t4, l), True, False)
            elif kind == "pflags":
                for k in range(4):
                    for j in range(4):
                        ins = g.tensor.matmul(ps[:, j:Q:4], T.fm[:, 16 - k:144 - k], T.gp[:, z * G + 4 * k + j:z * G + G:16], False, k + j == 6)
            elif kind == "prelu":
                out = own(T.tb3, l) if (r == RO - 1 and l < 3) else cut(T.gr, z, Q)
                if e == "V": ins = ts(out, ps[:, 0:Q], 0.0, None, A.max)
                else: ins = g.scalar.activation(out, ps[:, 0:Q], F.Relu)
            elif kind == "ppe": ins = compact(ps[:, 0:16], 4, T.gr, z * Q, 16)
            else: ins = move(e, mine(T["xl%d" % r], l) if r < RO - 1 else T.yts[:, 16 * q:16 * q + 16], ps[:, 0:16])
        elif kind == "hop3":
            r, l = a
            spread(name, mine(T["xl%d" % r], l) if r < RO - 1 else own(T.tb3, l) if l < 3 else T.yts[:, 16 * q:16 * q + 16])
        elif kind == "u":
            r, l, h = a
            at, c0 = P + G * l + H * h, 64 * l + 32 * h
            ins = move(e, T["u%d" % r][:, at:at + H], T["v%d" % r][:, 0:at + H].indirect(T["xl%d" % (r - 1)][:, c0:c0 + 32]))
        elif kind == "np":
            r, h = a
            x = T.tp16[:, 32 * h:32 * h + 32] if r == 0 else T.xl0[:, 192 + 32 * h:224 + 32 * h]
            ins = move(e, T["v%d" % (r + 1)][:, H * h:H * h + H], T["v%d" % r][:, 0:W].indirect(x))
        elif kind == "storet":
            ins = g.sync.dma_start(T.yt[:], T.yts[:])
        elif kind == "y0":
            ins = g.vector.tensor_copy(T["y%ss" % a[0][1]][:, 0:64], T[a[0] + "32"][:, 0:64])
        elif kind == "fgather":
            t, l, h = a
            at, c0 = ((l - 1) * 2 + (t == "fb")) * G + H * h, 64 * l + 32 * h
            ins = move(e, T.gf[:, at:at + H], T.tb3[:, 0:P + G * l].indirect(T[t + "16"][:, c0:c0 + 32]))
        elif kind == "fpe":
            t, l = a
            ins = compact(ps[:, 0:64], 4, T.gf, ((l - 1) * 2 + (t == "fb")) * G, 64)
        elif kind == "fcopy":
            t, l = a
            ins = move(e, T["y%ss" % t[1]][:, 64 * l:64 * l + 64], ps[:, 0:64])
        elif kind == "storey":
            t, c0, c1 = a
            ins = queue[e].dma_start(T["y" + t[1]][:, c0:c1], T["y%ss" % t[1]][:, c0:c1])
        if o["cost"] == "dma" or e == "Y":
            ins.then_inc(T.sem["s_" + name], 16)
            mark[name] = ("s_" + name, 16)
        elif o["cost"] == "hop":
            mark[name] = ("s_" + name, arrive)
        else:
            ins.then_inc(T.sem["c" + e], 1)
            count[e] += 1
            mark[name] = ("c" + e, count[e])
    mark["sent"] = ("sent", sent[0])
    wait("G", list(mark))
